import numpy as np
import ml_dtypes


def mxq(x, axis, fmt="e4m3"):
    dtype, down = {"e4m3": (ml_dtypes.float8_e4m3fn, 7), "e5m2": (ml_dtypes.float8_e5m2, 14)}[fmt]
    v = np.moveaxis(np.asarray(x, np.float32).astype(ml_dtypes.bfloat16).astype(np.float64), axis, -1)
    blocks = v.reshape(v.shape[:-1] + (-1, 32))
    amax = np.abs(blocks).max(-1, keepdims=True)
    byte = np.maximum(np.where(amax > 0, np.frexp(amax)[1] - 1 + 127, 0) - down, 1)
    scale = np.exp2(byte - 127.0)
    codes = (blocks / scale).astype(np.float32).astype(dtype).astype(np.float64)
    return np.moveaxis((codes * scale).reshape(v.shape), -1, axis)


WIDE = False


def mx_kscale(k):
    if not WIDE:
        return np.ones(k)
    levels = np.array([30, -30])
    if k % 512:
        return np.exp2(np.random.permutation(np.resize(levels, k // 32))).repeat(32)
    a = np.empty((k // 512, 16))
    for p in range(k // 512):
        a[p, :8] = np.random.permutation(np.resize(levels, 8))
        for g in range(8):
            far = levels[np.abs(levels - a[p, g]) >= 10]
            a[p, g + 8] = far[np.random.randint(len(far))]
    return np.exp2(a.ravel()).repeat(32)


def f64(x):
    return np.asarray(x).astype(np.float64)


def striped(idx):
    return np.tile(idx.reshape(-1, 16).T, (8, 1)).astype(np.uint16)


def unstriped(offs):
    return offs[:16].T.reshape(-1).astype(np.int64)


E2M1 = np.array([0.0, 0.5, 1.0, 1.5, 2.0, 3.0, 4.0, 6.0, -0.0, -0.5, -1.0, -1.5, -2.0, -3.0, -4.0, -6.0])


def pack_weight(w, fmt):
    k, n = w.shape
    w = f64(np.asarray(w, np.float32).astype(ml_dtypes.bfloat16)).reshape(k // 32, 32, n)
    amax = np.abs(w).max(1)
    if fmt == "e4m3":
        byte = np.frexp(amax)[1] - 1 + 127 - 7
    elif fmt == "e5m2":
        byte = np.frexp(amax)[1] - 1 + 127 - 14
    else:
        mant, ex = np.frexp(amax / 6.0)
        byte = np.where(mant > 0.5, ex, ex - 1) + 127
    byte = np.clip(np.where(amax > 0, byte, 1), 1, 254)
    scaled = (w * np.exp2(127.0 - byte)[:, None, :]).reshape(k, n).astype(np.float32)
    by_word = np.ascontiguousarray(scaled.reshape(k // 512, 128, 4, n).transpose(0, 1, 3, 2))
    if fmt == "e4m3":
        words = by_word.astype(ml_dtypes.float8_e4m3fn).view(np.uint8)
    elif fmt == "e5m2":
        words = by_word.astype(ml_dtypes.float8_e5m2).view(np.uint8)
    else:
        c = by_word.astype(ml_dtypes.float4_e2m1fn).view(np.uint8) & 0xF
        words = (c[..., 0::2] | (c[..., 1::2] << 4)).reshape(k // 512, 128, 2 * n)
    return np.ascontiguousarray(words), np.ascontiguousarray(byte.astype(np.uint8).reshape(k // 512, 16, n))


def unpack_weight(words, scales, fmt):
    g, _, n = scales.shape
    words = np.ascontiguousarray(words).reshape(g, 128, n, -1)
    if fmt == "e4m3":
        vals = words.view(ml_dtypes.float8_e4m3fn).astype(np.float64)
    elif fmt == "e5m2":
        vals = words.view(ml_dtypes.float8_e5m2).astype(np.float64)
    else:
        nib = np.empty((g, 128, n, 4), np.uint8)
        nib[..., 0::2] = words & 0xF
        nib[..., 1::2] = words >> 4
        vals = E2M1[nib]
    vals = vals * np.repeat(np.exp2(scales.astype(np.float64) - 127.0), 8, axis=1)[..., None]
    return vals.transpose(0, 1, 3, 2).reshape(g * 512, n)


def d_relu2(v):
    return 2.0 * np.maximum(v, 0.0)


K, T, E, C, H, N = 512, 1280, 5, 512, 512, 512


def by_expert(wq, xq):
    return np.concatenate([wq[e].T @ xq[:, e * C:(e + 1) * C] for e in range(E)], axis=1)


def setup_inputs():
    n = np.random.standard_normal
    s = mx_kscale(N)[:, None]
    u = mx_kscale(H)
    first = np.random.permutation(np.repeat(np.arange(E), T // E))
    second = (first + 1 + np.random.permutation(np.repeat(np.arange(E - 1), -(-T // (E - 1)))[:T])) % E
    while np.bincount(second, minlength=E).max() != T // E:
        load = np.bincount(second, minlength=E); hi, lo = int(load.argmax()), int(load.argmin())
        t = np.flatnonzero((second == hi) & (first != lo))[0]; second[t] = lo
    slot_token = np.empty(E * C, np.int64); pos = np.empty((2, T), np.int64); fill = np.zeros(E, np.int64)
    place = np.stack([np.random.permutation(C) for _ in range(E)])
    for r, deal in enumerate((first, second)):
        for t in np.random.permutation(T):
            e = deal[t]; j = e * C + place[e, fill[e]]; fill[e] += 1; slot_token[j] = t; pos[r, t] = j
    g = np.random.uniform(0.2, 0.8, T)
    w_slot = np.empty(E * C); w_slot[pos[0]] = g; w_slot[pos[1]] = 1.0 - g
    dy = pack_weight(n((N, T)) * s, "e5m2")
    return {
        "dy_words": dy[0],
        "dy_scales": dy[1],
        "a": n((H, E * C)).astype(np.float32),
        "w2": (n((E, N, H)) / np.sqrt(N) / s[None] * u[None, None, :]).astype(np.float32),
        "w1": (n((E, H, K)) / np.sqrt(H) / u[None, :, None]).astype(np.float32),
        "gate": np.tile(w_slot, (H, 1)).astype(np.float32),
        "offs": striped(slot_token),
        "pos1": striped(pos[0]),
        "pos2": striped(pos[1]),
    }


def reference(dy_words, dy_scales, a, w2, w1, gate, offs, pos1, pos2):
    idx = unstriped(offs)
    gq = unpack_weight(dy_words, dy_scales, "e5m2")[:, idx]
    dh = f64(gate) * by_expert(mxq(f64(w2), 1, "e4m3"), gq)
    da = dh * d_relu2(f64(a))
    dx = by_expert(mxq(f64(w1), 1, "e4m3"), mxq(da, 0, "e5m2"))
    return dx[:, unstriped(pos1)] + dx[:, unstriped(pos2)]

@@ -1,0 +1,197 @@
+from contextlib import ExitStack
+
+import concourse.mybir as mybir
+from concourse.masks import make_identity
+
+K, T, E, C, H, N = 512, 1280, 5, 512, 512, 512
+S = E * C
+FLOPS = 2 * S * (N * H + H * K)
+BYTES = 128 * T * 4 + 16 * T + 4 * (H * S + E * N * H + E * H * K + S + K * T) + 2 * 128 * (S + 2 * T) // 16
+
+F32 = mybir.dt.float32
+BF16 = mybir.dt.bfloat16
+I32 = mybir.dt.int32
+U32 = mybir.dt.uint32
+U16 = mybir.dt.uint16
+U8 = mybir.dt.uint8
+E4M3 = mybir.dt.float8_e4m3fn_x4
+E5M2 = mybir.dt.float8_e5m2_x4
+ALU = mybir.AluOpType
+COPY = mybir.ActivationFunctionType.Copy
+
+P = 128
+PACK = 4
+CHUNKS = C // P
+HALF = K // 2
+PIECE = T // 2
+
+
+def tile_moe_bdx_mlp_relu2_kernel(
+    tc, dy_words, dy_scales, a, w2, w1, gate, offs, pos1, pos2, out
+):
+    nc = tc.nc
+    with ExitStack() as ctx:
+        lists = ctx.enter_context(tc.tile_pool(name="lists", bufs=1))
+        keep = ctx.enter_context(tc.tile_pool(name="keep", bufs=1))
+        ring = ctx.enter_context(tc.tile_pool(name="ring", bufs=2))
+        psum = ctx.enter_context(tc.psum_pool(name="psum", bufs=1))
+
+        offs_sb = lists.tile([P, S // 16], U16, name="offs_sb")
+        pos1_sb = lists.tile([P, T // 16], U16, name="pos1_sb")
+        pos2_sb = lists.tile([P, T // 16], U16, name="pos2_sb")
+        dy_w = keep.tile([P, T], I32, name="dy_w", align_bytes=64)
+        dy_s = keep.tile([P, T], U8, name="dy_s", align_bytes=64)
+        gate_rows = keep.tile([P, P], F32, name="gate_rows", align_bytes=64)
+        gate2 = keep.tile([P, S // P], F32, name="gate2")
+        ident = keep.tile([P, P], F32, name="ident", align_bytes=64)
+
+        nc.gpsimd.memset(dy_s[:].bitcast(I32), 0)
+        nc.gpsimd.memset(gate_rows[:], 0.0)
+        make_identity(nc, ident[:])
+        nc.sync.dma_start(offs_sb[:], offs)
+        nc.sync.dma_start(pos1_sb[:], pos1)
+        nc.sync.dma_start(pos2_sb[:], pos2)
+        for r in range(4):
+            nc.sync.dma_start(dy_s[r:P:32, :].bitcast(I32), dy_scales[0, r:16:4, :].bitcast(I32))
+
+        w2_raw, a_sb, w1_raw = {}, {}, {}
+        w2_mx, dy_mx, da_mx, w1_mx = {}, {}, {}, {}
+
+        def load_w2(e):
+            w2_raw[e] = ring.tile([P, PACK, H], F32, name="w2_raw", tag="wide", bufs=E, align_bytes=64)
+            nc.sync.dma_start(w2_raw[e][:], w2[e].rearrange("(p j) i -> p j i", j=PACK))
+
+        def load_a(e):
+            a_sb[e] = ring.tile([P, PACK, C], F32, name="a_sb", bufs=E)
+            nc.sync.dma_start(a_sb[e][:], a[:, e * C : (e + 1) * C].rearrange("(p j) s -> p j s", j=PACK))
+
+        def load_w1(e, h):
+            w1_raw[e, h] = ring.tile([P, PACK, HALF], F32, name="w1_raw", bufs=2 * E)
+            nc.sync.dma_start(
+                w1_raw[e, h][:], w1[e][:, h * HALF : (h + 1) * HALF].rearrange("(p j) k -> p j k", j=PACK)
+            )
+
+        def interleave(copy, dst, src):
+            copy(dst.rearrange("p (c i) j -> p c j i", i=2), src.rearrange("p j (c i) -> p c j i", i=2))
+
+        def quantize(name, grouped, width, fmt, bufs):
+            codes = ring.tile([P, width], U32, name=name + "_codes", bufs=bufs, align_bytes=64)
+            scales = ring.tile([P, width], U8, name=name + "_scales", bufs=bufs, align_bytes=64)
+            nc.vector.quantize_mx(
+                out=codes[:].bitcast(fmt), scales=scales[:], in_=grouped[:].rearrange("p c j -> p (c j)")
+            )
+            return codes, scales
+
+        def gather(name, window, dtype, e):
+            got = ring.tile([P, C], dtype, name=name, bufs=E, align_bytes=64)
+            nc.vector.tensor_copy(got[:], window.indirect(offs_sb[:, e * C // 16 : (e + 1) * C // 16]))
+            return got
+
+        def prepare_w2(e):
+            grouped = ring.tile([P, H, PACK], BF16, name="w2_bf", tag="grouped", bufs=E, align_bytes=64)
+            for h in range(2):
+                cols = slice(h * H // 2, (h + 1) * H // 2)
+                copy = nc.vector.tensor_copy if (e, h) == (E - 1, 1) else nc.scalar.copy
+                interleave(copy, grouped[:, cols, :], w2_raw[e][:, :, cols])
+            w2_mx[e] = quantize("w2", grouped, H, E4M3, E)
+
+        def first_layer(e):
+            words, scales = dy_mx[e]
+            da = ring.tile([P, C, PACK], BF16, name="da", tag="grouped", bufs=E, align_bytes=64)
+            for c in range(CHUNKS):
+                cols = slice(c * P, (c + 1) * P)
+                sums = psum.tile([P, H], F32, name="sums", bufs=4)
+                nc.tensor.matmul_mx(
+                    out=sums[:],
+                    lhsT=words[:, cols].bitcast(E5M2),
+                    lhsT_scale=scales[:, cols],
+                    rhs=w2_mx[e][0][:].bitcast(E4M3),
+                    rhs_scale=w2_mx[e][1][:],
+                    start=True,
+                    stop=True,
+                )
+                dh = ring.tile([P, PACK, P], F32, name="dh", bufs=3, align_bytes=64)
+                col = e * CHUNKS + c
+                nc.scalar.activation(
+                    dh[:], sums[:].rearrange("s (p j) -> s j p", j=PACK), COPY, scale=gate2[:, col : col + 1]
+                )
+                turned = psum.tile([P, PACK, P], F32, name="turned", bufs=2)
+                for j in range(PACK):
+                    nc.tensor.transpose(turned[:, j, :], dh[:, j, :], ident[:])
+                nc.vector.scalar_tensor_tensor(
+                    out=da[:, cols, :],
+                    in0=a_sb[e][:, :, cols].rearrange("p j s -> p s j"),
+                    scalar=0.0,
+                    in1=turned[:].rearrange("p j s -> p s j"),
+                    op0=ALU.max,
+                    op1=ALU.mult,
+                )
+            da_mx[e] = quantize("da", da, C, E5M2, E)
+
+        def prepare_w1(e, kb):
+            grouped = ring.tile([P, P, PACK], BF16, name="w1_bf", bufs=E, align_bytes=64)
+            interleave(nc.scalar.copy, grouped[:], w1_raw[e, kb // 2][:, :, kb % 2 * P : (kb % 2 + 1) * P])
+            w1_mx[e, kb] = quantize("w1", grouped, P, E4M3, 2 * E)
+
+        def second_layer(e, kb):
+            codes, scales = w1_mx[e, kb]
+            acc = psum.tile([P, C], F32, name="acc", bufs=2)
+            nc.tensor.matmul_mx(
+                out=acc[:],
+                lhsT=codes[:].bitcast(E4M3),
+                lhsT_scale=scales[:],
+                rhs=da_mx[e][0][:].bitcast(E5M2),
+                rhs_scale=da_mx[e][1][:],
+                start=True,
+                stop=True,
+            )
+            nc.scalar.copy(dx[kb][:, e * C : (e + 1) * C], acc[:])
+
+        def combine(kb):
+            firsts = []
+            for u in range(T // PIECE):
+                first = ring.tile([P, PIECE], F32, name="first")
+                nc.vector.tensor_copy(first[:], dx[kb][:].indirect(pos1_sb[:, u * PIECE // 16 : (u + 1) * PIECE // 16]))
+                firsts.append(first)
+            for u in range(T // PIECE):
+                total = ring.tile([P, PIECE], F32, name="total", bufs=4)
+                nc.vector.tensor_tensor(
+                    total[:], dx[kb][:].indirect(pos2_sb[:, u * PIECE // 16 : (u + 1) * PIECE // 16]), firsts[u][:], ALU.add
+                )
+                nc.sync.dma_start(out[kb * P : (kb + 1) * P, u * PIECE : (u + 1) * PIECE], total[:])
+
+        for e in range(E):
+            if e == 2:
+                nc.sync.dma_start(dy_w[:], dy_words[0].rearrange("p t d -> p (t d)").bitcast(I32))
+            load_w2(e)
+        nc.sync.dma_start(gate_rows[0 : S // P, :], gate[0].rearrange("(c s) -> c s", s=P))
+        gate_t = psum.tile([P, PACK, P], F32, name="turned", bufs=2)
+        nc.tensor.transpose(gate_t[:, 0, :], gate_rows[:], ident[:])
+        nc.scalar.activation(gate2[:], gate_t[:, 0, 0 : S // P], COPY, scale=2.0)
+        for e in range(E):
+            load_a(e)
+            load_w1(e, 0)
+        for e in range(E):
+            load_w1(e, 1)
+        g_scales = [gather("g_scales", dy_s[:], U8, e) for e in range(E)]
+        g_words = [gather("g_words", dy_w[:].bitcast(U32), U32, e) for e in range(E)]
+        for e in range(E):
+            dy_mx[e] = g_words[e], g_scales[e]
+            prepare_w2(e)
+        dx = [ring.tile([P, S], F32, name="dx", tag="wide", bufs=E, align_bytes=64) for kb in range(K // P)]
+        for e in range(E):
+            first_layer(e)
+            prepare_w1(e, 0)
+            if e + 1 < E:
+                second_layer(e, 0)
+        for e in range(E):
+            prepare_w1(e, 1)
+        second_layer(E - 1, 0)
+        for kb in range(K // P):
+            if kb + 2 < K // P:
+                for e in range(E):
+                    prepare_w1(e, kb + 2)
+            combine(kb)
+            if kb + 1 < K // P:
+                for e in range(E):
+                    second_layer(e, kb + 1)

@@ -23,7 +23,6 @@ P = 128
 PACK = 4
 CHUNKS = C // P
 HALF = K // 2
-PIECE = T // 2
 
 
 def tile_moe_bdx_mlp_relu2_kernel(
@@ -58,7 +57,7 @@ def tile_moe_bdx_mlp_relu2_kernel(
         w2_mx, dy_mx, da_mx, w1_mx = {}, {}, {}, {}
 
         def load_w2(e):
-            w2_raw[e] = ring.tile([P, PACK, H], F32, name="w2_raw", tag="wide", bufs=E, align_bytes=64)
+            w2_raw[e] = ring.tile([P, PACK, H], F32, name="w2_raw", tag="rows", bufs=E, align_bytes=64)
             nc.sync.dma_start(w2_raw[e][:], w2[e].rearrange("(p j) i -> p j i", j=PACK))
 
         def load_a(e):
@@ -91,16 +90,16 @@ def tile_moe_bdx_mlp_relu2_kernel(
             grouped = ring.tile([P, H, PACK], BF16, name="w2_bf", tag="grouped", bufs=E, align_bytes=64)
             for h in range(2):
                 cols = slice(h * H // 2, (h + 1) * H // 2)
-                copy = nc.vector.tensor_copy if (e, h) == (E - 1, 1) else nc.scalar.copy
+                copy = nc.vector.tensor_copy if e == E - 1 else nc.scalar.copy
                 interleave(copy, grouped[:, cols, :], w2_raw[e][:, :, cols])
-            w2_mx[e] = quantize("w2", grouped, H, E4M3, E)
+            w2_mx[e] = quantize("wide", grouped, H, E4M3, E)
 
         def first_layer(e):
             words, scales = dy_mx[e]
             da = ring.tile([P, C, PACK], BF16, name="da", tag="grouped", bufs=E, align_bytes=64)
             for c in range(CHUNKS):
                 cols = slice(c * P, (c + 1) * P)
-                sums = psum.tile([P, H], F32, name="sums", bufs=4)
+                sums = psum.tile([P, H], F32, name="sums", tag="sums", bufs=4)
                 nc.tensor.matmul_mx(
                     out=sums[:],
                     lhsT=words[:, cols].bitcast(E5M2),
@@ -115,7 +114,7 @@ def tile_moe_bdx_mlp_relu2_kernel(
                 nc.scalar.activation(
                     dh[:], sums[:].rearrange("s (p j) -> s j p", j=PACK), COPY, scale=gate2[:, col : col + 1]
                 )
-                turned = psum.tile([P, PACK, P], F32, name="turned", bufs=2)
+                turned = psum.tile([P, PACK, P], F32, name="turned", bufs=3)
                 for j in range(PACK):
                     nc.tensor.transpose(turned[:, j, :], dh[:, j, :], ident[:])
                 nc.vector.scalar_tensor_tensor(
@@ -128,18 +127,31 @@ def tile_moe_bdx_mlp_relu2_kernel(
                 )
             da_mx[e] = quantize("da", da, C, E5M2, E)
 
-        def prepare_w1(e, kb):
-            grouped = ring.tile([P, P, PACK], BF16, name="w1_bf", bufs=E, align_bytes=64)
-            interleave(nc.scalar.copy, grouped[:], w1_raw[e, kb // 2][:, :, kb % 2 * P : (kb % 2 + 1) * P])
-            w1_mx[e, kb] = quantize("w1", grouped, P, E4M3, 2 * E)
+        def prepare_w1(experts, kb):
+            tag, name = ("grouped", "wide") if len(experts) > 1 else ("w1_bf", "narrow")
+            grouped = ring.tile([P, len(experts) * P, PACK], BF16, name="w1_bf", tag=tag, bufs=E, align_bytes=64)
+            for n, e in enumerate(experts):
+                interleave(
+                    nc.scalar.copy,
+                    grouped[:, n * P : (n + 1) * P, :],
+                    w1_raw[e, kb // 2][:, :, kb % 2 * P : (kb % 2 + 1) * P],
+                )
+            codes, scales = quantize(name, grouped, len(experts) * P, E4M3, E)
+            for n, e in enumerate(experts):
+                w1_mx[e, kb] = codes[:, n * P : (n + 1) * P], scales[:, n * P : (n + 1) * P]
+
+        def prepare_w1_block(kb):
+            prepare_w1(list(range(E - 1)), kb)
+            prepare_w1([E - 1], kb)
 
         def second_layer(e, kb):
             codes, scales = w1_mx[e, kb]
-            acc = psum.tile([P, C], F32, name="acc", bufs=2)
+            tag, bufs = ("acc", 1) if kb == 0 else ("sums", 4)
+            acc = psum.tile([P, C], F32, name="acc", tag=tag, bufs=bufs)
             nc.tensor.matmul_mx(
                 out=acc[:],
-                lhsT=codes[:].bitcast(E4M3),
-                lhsT_scale=scales[:],
+                lhsT=codes.bitcast(E4M3),
+                lhsT_scale=scales,
                 rhs=da_mx[e][0][:].bitcast(E5M2),
                 rhs_scale=da_mx[e][1][:],
                 start=True,
@@ -148,28 +160,30 @@ def tile_moe_bdx_mlp_relu2_kernel(
             nc.scalar.copy(dx[kb][:, e * C : (e + 1) * C], acc[:])
 
         def combine(kb):
+            cuts = [0, T // 2, T] if kb + 1 < K // P else [0, T // 2, 3 * T // 4, T]
+            pieces = list(zip(cuts, cuts[1:]))
             firsts = []
-            for u in range(T // PIECE):
-                first = ring.tile([P, PIECE], F32, name="first")
-                nc.vector.tensor_copy(first[:], dx[kb][:].indirect(pos1_sb[:, u * PIECE // 16 : (u + 1) * PIECE // 16]))
+            for lo, hi in pieces:
+                first = ring.tile([P, hi - lo], F32, name="first", bufs=3)
+                nc.vector.tensor_copy(first[:], dx[kb][:].indirect(pos1_sb[:, lo // 16 : hi // 16]))
                 firsts.append(first)
-            for u in range(T // PIECE):
-                total = ring.tile([P, PIECE], F32, name="total", bufs=4)
-                nc.vector.tensor_tensor(
-                    total[:], dx[kb][:].indirect(pos2_sb[:, u * PIECE // 16 : (u + 1) * PIECE // 16]), firsts[u][:], ALU.add
-                )
-                nc.sync.dma_start(out[kb * P : (kb + 1) * P, u * PIECE : (u + 1) * PIECE], total[:])
+            for (lo, hi), first in zip(pieces, firsts):
+                total = ring.tile([P, hi - lo], F32, name="total", bufs=4)
+                nc.vector.tensor_tensor(total[:], dx[kb][:].indirect(pos2_sb[:, lo // 16 : hi // 16]), first[:], ALU.add)
+                nc.sync.dma_start(out[kb * P : (kb + 1) * P, lo:hi], total[:])
 
-        for e in range(E):
+        for e in range(E - 1):
             if e == 2:
                 nc.sync.dma_start(dy_w[:], dy_words[0].rearrange("p t d -> p (t d)").bitcast(I32))
             load_w2(e)
         nc.sync.dma_start(gate_rows[0 : S // P, :], gate[0].rearrange("(c s) -> c s", s=P))
-        gate_t = psum.tile([P, PACK, P], F32, name="turned", bufs=2)
+        gate_t = psum.tile([P, PACK, P], F32, name="turned", bufs=3)
         nc.tensor.transpose(gate_t[:, 0, :], gate_rows[:], ident[:])
         nc.scalar.activation(gate2[:], gate_t[:, 0, 0 : S // P], COPY, scale=2.0)
         for e in range(E):
             load_a(e)
+            if e == 0:
+                load_w2(E - 1)
             load_w1(e, 0)
         for e in range(E):
             load_w1(e, 1)
@@ -178,19 +192,17 @@ def tile_moe_bdx_mlp_relu2_kernel(
         for e in range(E):
             dy_mx[e] = g_words[e], g_scales[e]
             prepare_w2(e)
-        dx = [ring.tile([P, S], F32, name="dx", tag="wide", bufs=E, align_bytes=64) for kb in range(K // P)]
+        dx = [ring.tile([P, S], F32, name="dx", tag="rows", bufs=E, align_bytes=64) for kb in range(K // P)]
         for e in range(E):
             first_layer(e)
-            prepare_w1(e, 0)
+            prepare_w1([e], 0)
             if e + 1 < E:
                 second_layer(e, 0)
-        for e in range(E):
-            prepare_w1(e, 1)
+        prepare_w1_block(1)
         second_layer(E - 1, 0)
         for kb in range(K // P):
             if kb + 2 < K // P:
-                for e in range(E):
-                    prepare_w1(e, kb + 2)
+                prepare_w1_block(kb + 2)
             combine(kb)
             if kb + 1 < K // P:
                 for e in range(E):

@@ -23,6 +23,15 @@ P = 128
 PACK = 4
 CHUNKS = C // P
 HALF = K // 2
+RELU = 0
+W2V = 1
+W2G = 0
+NEAR = 0
+SUMS, TURN, ACC = 4, 4, 0
+DH = 4
+LOADS = "w0 w1 d w2 w3 g a0 w4 n0 a1 n1 a2 n2 a3 n3 a4 n4 f0 f1 f2 f3 f4"
+RP = 2
+POS = 3
 
 
 def tile_moe_bdx_mlp_relu2_kernel(
@@ -64,6 +73,11 @@ def tile_moe_bdx_mlp_relu2_kernel(
             a_sb[e] = ring.tile([P, PACK, C], F32, name="a_sb", bufs=E)
             nc.sync.dma_start(a_sb[e][:], a[:, e * C : (e + 1) * C].rearrange("(p j) s -> p j s", j=PACK))
 
+        def relu(e):
+            for h in range(RP):
+                part = a_sb[e][:, :, h * C // RP : (h + 1) * C // RP]
+                nc.gpsimd.tensor_scalar(part, part, 0.0, 1.0, ALU.max, ALU.mult)
+
         def load_w1(e, h):
             w1_raw[e, h] = ring.tile([P, PACK, HALF], F32, name="w1_raw", bufs=2 * E)
             nc.sync.dma_start(
@@ -73,12 +87,16 @@ def tile_moe_bdx_mlp_relu2_kernel(
         def interleave(copy, dst, src):
             copy(dst.rearrange("p (c i) j -> p c j i", i=2), src.rearrange("p j (c i) -> p c j i", i=2))
 
-        def quantize(name, grouped, width, fmt, bufs):
+        def quantize(name, grouped, width, fmt, bufs, parts=1):
             codes = ring.tile([P, width], U32, name=name + "_codes", bufs=bufs, align_bytes=64)
             scales = ring.tile([P, width], U8, name=name + "_scales", bufs=bufs, align_bytes=64)
-            nc.vector.quantize_mx(
-                out=codes[:].bitcast(fmt), scales=scales[:], in_=grouped[:].rearrange("p c j -> p (c j)")
-            )
+            for h in range(parts):
+                cols = slice(h * width // parts, (h + 1) * width // parts)
+                nc.vector.quantize_mx(
+                    out=codes[:, cols].bitcast(fmt),
+                    scales=scales[:, cols],
+                    in_=grouped[:, cols, :].rearrange("p c j -> p (c j)"),
+                )
             return codes, scales
 
         def gather(name, window, dtype, e):
@@ -90,8 +108,12 @@ def tile_moe_bdx_mlp_relu2_kernel(
             grouped = ring.tile([P, H, PACK], BF16, name="w2_bf", tag="grouped", bufs=E, align_bytes=64)
             for h in range(2):
                 cols = slice(h * H // 2, (h + 1) * H // 2)
-                copy = nc.vector.tensor_copy if e == E - 1 else nc.scalar.copy
-                interleave(copy, grouped[:, cols, :], w2_raw[e][:, :, cols])
+                if e >= E - W2G:
+                    src = w2_raw[e][:, :, cols].rearrange("p j k -> p k j")
+                    nc.gpsimd.tensor_scalar(grouped[:, cols, :], src, 1.0, 0.0, ALU.mult, ALU.add)
+                else:
+                    copy = nc.vector.tensor_copy if e >= E - W2V else nc.scalar.copy
+                    interleave(copy, grouped[:, cols, :], w2_raw[e][:, :, cols])
             w2_mx[e] = quantize("wide", grouped, H, E4M3, E)
 
         def first_layer(e):
@@ -99,7 +121,7 @@ def tile_moe_bdx_mlp_relu2_kernel(
             da = ring.tile([P, C, PACK], BF16, name="da", tag="grouped", bufs=E, align_bytes=64)
             for c in range(CHUNKS):
                 cols = slice(c * P, (c + 1) * P)
-                sums = psum.tile([P, H], F32, name="sums", tag="sums", bufs=4)
+                sums = psum.tile([P, H], F32, name="sums", tag="sums", bufs=SUMS)
                 nc.tensor.matmul_mx(
                     out=sums[:],
                     lhsT=words[:, cols].bitcast(E5M2),
@@ -109,23 +131,33 @@ def tile_moe_bdx_mlp_relu2_kernel(
                     start=True,
                     stop=True,
                 )
-                dh = ring.tile([P, PACK, P], F32, name="dh", bufs=3, align_bytes=64)
+                dh = ring.tile([P, PACK, P], F32, name="dh", bufs=DH, align_bytes=64)
                 col = e * CHUNKS + c
                 nc.scalar.activation(
                     dh[:], sums[:].rearrange("s (p j) -> s j p", j=PACK), COPY, scale=gate2[:, col : col + 1]
                 )
-                turned = psum.tile([P, PACK, P], F32, name="turned", bufs=3)
+                turned = psum.tile([P, PACK, P], F32, name="turned", tag="turned", bufs=TURN)
                 for j in range(PACK):
                     nc.tensor.transpose(turned[:, j, :], dh[:, j, :], ident[:])
-                nc.vector.scalar_tensor_tensor(
-                    out=da[:, cols, :],
-                    in0=a_sb[e][:, :, cols].rearrange("p j s -> p s j"),
-                    scalar=0.0,
-                    in1=turned[:].rearrange("p j s -> p s j"),
-                    op0=ALU.max,
-                    op1=ALU.mult,
-                )
-            da_mx[e] = quantize("da", da, C, E5M2, E)
+                if c == POS and e > 0:
+                    second_layer(e - 1, 0)
+                if e < RELU:
+                    nc.vector.tensor_tensor(
+                        da[:, cols, :].rearrange("p (c i) j -> p c j i", i=2),
+                        turned[:].rearrange("p j (c i) -> p c j i", i=2),
+                        a_sb[e][:, :, cols].rearrange("p j (c i) -> p c j i", i=2),
+                        ALU.mult,
+                    )
+                else:
+                    nc.vector.scalar_tensor_tensor(
+                        out=da[:, cols, :],
+                        in0=a_sb[e][:, :, cols].rearrange("p j s -> p s j"),
+                        scalar=0.0,
+                        in1=turned[:].rearrange("p j s -> p s j"),
+                        op0=ALU.max,
+                        op1=ALU.mult,
+                    )
+            da_mx[e] = quantize("da", da, C, E5M2, E, 2)
 
         def prepare_w1(experts, kb):
             tag, name = ("grouped", "wide") if len(experts) > 1 else ("w1_bf", "narrow")
@@ -146,7 +178,7 @@ def tile_moe_bdx_mlp_relu2_kernel(
 
         def second_layer(e, kb):
             codes, scales = w1_mx[e, kb]
-            tag, bufs = ("acc", 1) if kb == 0 else ("sums", 4)
+            tag, bufs = ("turned", TURN) if kb == 0 else ("sums", SUMS)
             acc = psum.tile([P, C], F32, name="acc", tag=tag, bufs=bufs)
             nc.tensor.matmul_mx(
                 out=acc[:],
@@ -172,21 +204,22 @@ def tile_moe_bdx_mlp_relu2_kernel(
                 nc.vector.tensor_tensor(total[:], dx[kb][:].indirect(pos2_sb[:, lo // 16 : hi // 16]), first[:], ALU.add)
                 nc.sync.dma_start(out[kb * P : (kb + 1) * P, lo:hi], total[:])
 
-        for e in range(E - 1):
-            if e == 2:
+        for item in LOADS.split():
+            if item == "d":
                 nc.sync.dma_start(dy_w[:], dy_words[0].rearrange("p t d -> p (t d)").bitcast(I32))
-            load_w2(e)
-        nc.sync.dma_start(gate_rows[0 : S // P, :], gate[0].rearrange("(c s) -> c s", s=P))
-        gate_t = psum.tile([P, PACK, P], F32, name="turned", bufs=3)
-        nc.tensor.transpose(gate_t[:, 0, :], gate_rows[:], ident[:])
-        nc.scalar.activation(gate2[:], gate_t[:, 0, 0 : S // P], COPY, scale=2.0)
-        for e in range(E):
-            load_a(e)
-            if e == 0:
-                load_w2(E - 1)
-            load_w1(e, 0)
-        for e in range(E):
-            load_w1(e, 1)
+            elif item == "g":
+                nc.sync.dma_start(gate_rows[0 : S // P, :], gate[0].rearrange("(c s) -> c s", s=P))
+                gate_t = psum.tile([P, PACK, P], F32, name="turned", tag="turned", bufs=TURN)
+                nc.tensor.transpose(gate_t[:, 0, :], gate_rows[:], ident[:])
+                nc.scalar.activation(gate2[:], gate_t[:, 0, 0 : S // P], COPY, scale=2.0)
+            elif item[0] == "w":
+                load_w2(int(item[1]))
+            elif item[0] == "a":
+                load_a(int(item[1]))
+            else:
+                load_w1(int(item[1]), 0 if item[0] == "n" else 1)
+        for e in range(RELU):
+            relu(e)
         g_scales = [gather("g_scales", dy_s[:], U8, e) for e in range(E)]
         g_words = [gather("g_words", dy_w[:].bitcast(U32), U32, e) for e in range(E)]
         for e in range(E):
@@ -196,8 +229,6 @@ def tile_moe_bdx_mlp_relu2_kernel(
         for e in range(E):
             first_layer(e)
             prepare_w1([e], 0)
-            if e + 1 < E:
-                second_layer(e, 0)
         prepare_w1_block(1)
         second_layer(E - 1, 0)
         for kb in range(K // P):

@@ -31,6 +31,7 @@ SUMS, TURN, ACC = 4, 4, 0
 DH = 4
 LOADS = "w0 w1 d w2 w3 g a0 w4 n0 a1 n1 a2 n2 a3 n3 a4 n4 f0 f1 f2 f3 f4"
 RP = 2
+STAGGER = 9
 POS = 3
 
 
@@ -70,8 +71,9 @@ def tile_moe_bdx_mlp_relu2_kernel(
             nc.sync.dma_start(w2_raw[e][:], w2[e].rearrange("(p j) i -> p j i", j=PACK))
 
         def load_a(e):
-            a_sb[e] = ring.tile([P, PACK, C], F32, name="a_sb", bufs=E)
-            nc.sync.dma_start(a_sb[e][:], a[:, e * C : (e + 1) * C].rearrange("(p j) s -> p j s", j=PACK))
+            padded = ring.tile([P, PACK, C + STAGGER], F32, name="a_sb", bufs=E)
+            a_sb[e] = padded[:, :, 0:C]
+            nc.sync.dma_start(a_sb[e], a[:, e * C : (e + 1) * C].rearrange("(p j) s -> p j s", j=PACK))
 
         def relu(e):
             for h in range(RP):

@@ -31,7 +31,8 @@ SUMS, TURN, ACC = 4, 4, 0
 DH = 4
 LOADS = "w0 w1 d w2 w3 g a0 w4 n0 a1 n1 a2 n2 a3 n3 a4 n4 f0 f1 f2 f3 f4"
 RP = 2
-STAGGER = 9
+NOW = 0
+STAGGER = 0
 POS = 3
 
 
@@ -58,10 +59,10 @@ def tile_moe_bdx_mlp_relu2_kernel(
         nc.gpsimd.memset(gate_rows[:], 0.0)
         make_identity(nc, ident[:])
         nc.sync.dma_start(offs_sb[:], offs)
-        nc.sync.dma_start(pos1_sb[:], pos1)
-        nc.sync.dma_start(pos2_sb[:], pos2)
         for r in range(4):
             nc.sync.dma_start(dy_s[r:P:32, :].bitcast(I32), dy_scales[0, r:16:4, :].bitcast(I32))
+        nc.sync.dma_start(pos1_sb[:], pos1)
+        nc.sync.dma_start(pos2_sb[:], pos2)
 
         w2_raw, a_sb, w1_raw = {}, {}, {}
         w2_mx, dy_mx, da_mx, w1_mx = {}, {}, {}, {}
@@ -107,7 +108,7 @@ def tile_moe_bdx_mlp_relu2_kernel(
             return got
 
         def prepare_w2(e):
-            grouped = ring.tile([P, H, PACK], BF16, name="w2_bf", tag="grouped", bufs=E, align_bytes=64)
+            grouped = ring.tile([P, H, PACK], BF16, name="w2_bf", tag="grouped", bufs=E - 1, align_bytes=64)
             for h in range(2):
                 cols = slice(h * H // 2, (h + 1) * H // 2)
                 if e >= E - W2G:
@@ -120,7 +121,7 @@ def tile_moe_bdx_mlp_relu2_kernel(
 
         def first_layer(e):
             words, scales = dy_mx[e]
-            da = ring.tile([P, C, PACK], BF16, name="da", tag="grouped", bufs=E, align_bytes=64)
+            da = ring.tile([P, C, PACK], BF16, name="da", tag="da", bufs=2, align_bytes=64)
             for c in range(CHUNKS):
                 cols = slice(c * P, (c + 1) * P)
                 sums = psum.tile([P, H], F32, name="sums", tag="sums", bufs=SUMS)
@@ -141,8 +142,8 @@ def tile_moe_bdx_mlp_relu2_kernel(
                 turned = psum.tile([P, PACK, P], F32, name="turned", tag="turned", bufs=TURN)
                 for j in range(PACK):
                     nc.tensor.transpose(turned[:, j, :], dh[:, j, :], ident[:])
-                if c == POS and e > 0:
-                    second_layer(e - 1, 0)
+                if c == POS and 0 < e <= NOW:
+                    second_layer(e - 1, 0, "turned", TURN)
                 if e < RELU:
                     nc.vector.tensor_tensor(
                         da[:, cols, :].rearrange("p (c i) j -> p c j i", i=2),
@@ -161,16 +162,16 @@ def tile_moe_bdx_mlp_relu2_kernel(
                     )
             da_mx[e] = quantize("da", da, C, E5M2, E, 2)
 
-        def prepare_w1(experts, kb):
-            tag, name = ("grouped", "wide") if len(experts) > 1 else ("w1_bf", "narrow")
-            grouped = ring.tile([P, len(experts) * P, PACK], BF16, name="w1_bf", tag=tag, bufs=E, align_bytes=64)
+        def prepare_w1(experts, kb, copy=nc.scalar.copy):
+            tag, name, bufs = {1: ("w1_bf", "narrow", E), 2: ("da", "pair", 2), 4: ("grouped", "wide", E - 1)}[len(experts)]
+            grouped = ring.tile([P, len(experts) * P, PACK], BF16, name="w1_bf", tag=tag, bufs=bufs, align_bytes=64)
             for n, e in enumerate(experts):
                 interleave(
-                    nc.scalar.copy,
+                    copy,
                     grouped[:, n * P : (n + 1) * P, :],
                     w1_raw[e, kb // 2][:, :, kb % 2 * P : (kb % 2 + 1) * P],
                 )
-            codes, scales = quantize(name, grouped, len(experts) * P, E4M3, E)
+            codes, scales = quantize(name, grouped, len(experts) * P, E4M3, 2 if name == "pair" else E)
             for n, e in enumerate(experts):
                 w1_mx[e, kb] = codes[:, n * P : (n + 1) * P], scales[:, n * P : (n + 1) * P]
 
@@ -178,9 +179,8 @@ def tile_moe_bdx_mlp_relu2_kernel(
             prepare_w1(list(range(E - 1)), kb)
             prepare_w1([E - 1], kb)
 
-        def second_layer(e, kb):
+        def second_layer(e, kb, tag="sums", bufs=SUMS):
             codes, scales = w1_mx[e, kb]
-            tag, bufs = ("turned", TURN) if kb == 0 else ("sums", SUMS)
             acc = psum.tile([P, C], F32, name="acc", tag=tag, bufs=bufs)
             nc.tensor.matmul_mx(
                 out=acc[:],
@@ -194,16 +194,16 @@ def tile_moe_bdx_mlp_relu2_kernel(
             nc.scalar.copy(dx[kb][:, e * C : (e + 1) * C], acc[:])
 
         def combine(kb):
-            cuts = [0, T // 2, T] if kb + 1 < K // P else [0, T // 2, 3 * T // 4, T]
-            pieces = list(zip(cuts, cuts[1:]))
+            cuts = [0, T // 2, T] if kb + 1 < K // P else [0, T // 2, T - 256, T - 128, T]
             firsts = []
-            for lo, hi in pieces:
-                first = ring.tile([P, hi - lo], F32, name="first", bufs=3)
-                nc.vector.tensor_copy(first[:], dx[kb][:].indirect(pos1_sb[:, lo // 16 : hi // 16]))
+            for lo in (0, T // 2):
+                first = ring.tile([P, T // 2], F32, name="first", bufs=3)
+                nc.vector.tensor_copy(first[:], dx[kb][:].indirect(pos1_sb[:, lo // 16 : (lo + T // 2) // 16]))
                 firsts.append(first)
-            for (lo, hi), first in zip(pieces, firsts):
+            for lo, hi in zip(cuts, cuts[1:]):
+                first = firsts[lo // (T // 2)][:, lo % (T // 2) : lo % (T // 2) + hi - lo]
                 total = ring.tile([P, hi - lo], F32, name="total", bufs=4)
-                nc.vector.tensor_tensor(total[:], dx[kb][:].indirect(pos2_sb[:, lo // 16 : hi // 16]), first[:], ALU.add)
+                nc.vector.tensor_tensor(total[:], dx[kb][:].indirect(pos2_sb[:, lo // 16 : hi // 16]), first, ALU.add)
                 nc.sync.dma_start(out[kb * P : (kb + 1) * P, lo:hi], total[:])
 
         for item in LOADS.split():
@@ -231,8 +231,12 @@ def tile_moe_bdx_mlp_relu2_kernel(
         for e in range(E):
             first_layer(e)
             prepare_w1([e], 0)
-        prepare_w1_block(1)
-        second_layer(E - 1, 0)
+        for e in range(NOW, E - 1):
+            second_layer(e, 0)
+        prepare_w1([2], 1)
+        prepare_w1([0, 1], 1)
+        prepare_w1([3, 4], 1, nc.vector.tensor_copy)
+        second_layer(E - 1, 0, "turned", TURN)
         for kb in range(K // P):
             if kb + 2 < K // P:
                 prepare_w1_block(kb + 2)

@@ -23,7 +23,9 @@ P = 128
 PACK = 4
 CHUNKS = C // P
 HALF = K // 2
-RELU = 0
+RC = 1
+R0 = 1
+RELU = mybir.ActivationFunctionType.Relu
 W2V = 1
 W2G = 0
 NEAR = 0
@@ -75,11 +77,6 @@ def tile_moe_bdx_mlp_relu2_kernel(
             padded = ring.tile([P, PACK, C + STAGGER], F32, name="a_sb", bufs=E)
             a_sb[e] = padded[:, :, 0:C]
             nc.sync.dma_start(a_sb[e], a[:, e * C : (e + 1) * C].rearrange("(p j) s -> p j s", j=PACK))
-
-        def relu(e):
-            for h in range(RP):
-                part = a_sb[e][:, :, h * C // RP : (h + 1) * C // RP]
-                nc.gpsimd.tensor_scalar(part, part, 0.0, 1.0, ALU.max, ALU.mult)
 
         def load_w1(e, h):
             w1_raw[e, h] = ring.tile([P, PACK, HALF], F32, name="w1_raw", bufs=2 * E)
@@ -144,13 +141,14 @@ def tile_moe_bdx_mlp_relu2_kernel(
                     nc.tensor.transpose(turned[:, j, :], dh[:, j, :], ident[:])
                 if c == POS and 0 < e <= NOW:
                     second_layer(e - 1, 0, "turned", TURN)
-                if e < RELU:
-                    nc.vector.tensor_tensor(
-                        da[:, cols, :].rearrange("p (c i) j -> p c j i", i=2),
-                        turned[:].rearrange("p j (c i) -> p c j i", i=2),
+                if e >= R0 and c >= CHUNKS - RC:
+                    slope = ring.tile([P, P, PACK], F32, name="slope", bufs=RC, align_bytes=64)
+                    nc.scalar.activation(
+                        slope[:].rearrange("p (c i) j -> p c j i", i=2),
                         a_sb[e][:, :, cols].rearrange("p j (c i) -> p c j i", i=2),
-                        ALU.mult,
+                        RELU,
                     )
+                    nc.vector.tensor_tensor(da[:, cols, :], turned[:].rearrange("p j s -> p s j"), slope[:], ALU.mult)
                 else:
                     nc.vector.scalar_tensor_tensor(
                         out=da[:, cols, :],
@@ -220,8 +218,6 @@ def tile_moe_bdx_mlp_relu2_kernel(
                 load_a(int(item[1]))
             else:
                 load_w1(int(item[1]), 0 if item[0] == "n" else 1)
-        for e in range(RELU):
-            relu(e)
         g_scales = [gather("g_scales", dy_s[:], U8, e) for e in range(E)]
         g_words = [gather("g_words", dy_w[:].bitcast(U32), U32, e) for e in range(E)]
         for e in range(E):

@@ -22,20 +22,16 @@ COPY = mybir.ActivationFunctionType.Copy
 P = 128
 PACK = 4
 CHUNKS = C // P
-HALF = K // 2
-RC = 1
-R0 = 1
-RELU = mybir.ActivationFunctionType.Relu
-W2V = 1
-W2G = 0
-NEAR = 0
-SUMS, TURN, ACC = 4, 4, 0
-DH = 4
-LOADS = "w0 w1 d w2 w3 g a0 w4 n0 a1 n1 a2 n2 a3 n3 a4 n4 f0 f1 f2 f3 f4"
-RP = 2
-NOW = 0
-STAGGER = 0
-POS = 3
+BLOCKS = K // P
+HOP = 1
+FLOAT_MAX = 3.4028234663852886e38
+LOADS = "w0 w1 d g b0 w2 c0 w3 a1 w4 a2 q0 q1 q2 q3 a3 a4 q4 r0 r1 r2 r3 r4 f0 f1 f2 f3 f4"
+
+HEAD = 10240
+PERIOD = 8192
+ROUNDED, WORDS, SLOPE, DA, CODES = 0, 0, 2048, 3584, 4096
+A_ROWS = HEAD + (E + 1) * PERIOD
+W_ROWS = A_ROWS + E * 8192
 
 
 def tile_moe_bdx_mlp_relu2_kernel(
@@ -45,15 +41,21 @@ def tile_moe_bdx_mlp_relu2_kernel(
     with ExitStack() as ctx:
         lists = ctx.enter_context(tc.tile_pool(name="lists", bufs=1))
         keep = ctx.enter_context(tc.tile_pool(name="keep", bufs=1))
-        ring = ctx.enter_context(tc.tile_pool(name="ring", bufs=2))
+        laid = ctx.enter_context(tc.tile_pool(name="laid", bufs=1))
         psum = ctx.enter_context(tc.psum_pool(name="psum", bufs=1))
+
+        def place(name, shape, dtype, offset):
+            return laid.tile(shape, dtype, name=name, offset=offset, align_bytes=64)
+
+        def period(e):
+            return HEAD + (e + 1) * PERIOD
 
         offs_sb = lists.tile([P, S // 16], U16, name="offs_sb")
         pos1_sb = lists.tile([P, T // 16], U16, name="pos1_sb")
         pos2_sb = lists.tile([P, T // 16], U16, name="pos2_sb")
         dy_w = keep.tile([P, T], I32, name="dy_w", align_bytes=64)
         dy_s = keep.tile([P, T], U8, name="dy_s", align_bytes=64)
-        gate_rows = keep.tile([P, P], F32, name="gate_rows", align_bytes=64)
+        gate_rows = place("gate_rows", [P, P], F32, W_ROWS + E * 8192)
         gate2 = keep.tile([P, S // P], F32, name="gate2")
         ident = keep.tile([P, P], F32, name="ident", align_bytes=64)
 
@@ -67,121 +69,125 @@ def tile_moe_bdx_mlp_relu2_kernel(
         nc.sync.dma_start(pos2_sb[:], pos2)
 
         w2_raw, a_sb, w1_raw = {}, {}, {}
-        w2_mx, dy_mx, da_mx, w1_mx = {}, {}, {}, {}
+        w2_mx, g_words, g_scales, da, da_mx, w1_mx = {}, {}, {}, {}, {}, {}
 
-        def load_w2(e):
-            w2_raw[e] = ring.tile([P, PACK, H], F32, name="w2_raw", tag="rows", bufs=E, align_bytes=64)
-            nc.sync.dma_start(w2_raw[e][:], w2[e].rearrange("(p j) i -> p j i", j=PACK))
-
-        def load_a(e):
-            padded = ring.tile([P, PACK, C + STAGGER], F32, name="a_sb", bufs=E)
-            a_sb[e] = padded[:, :, 0:C]
-            nc.sync.dma_start(a_sb[e], a[:, e * C : (e + 1) * C].rearrange("(p j) s -> p j s", j=PACK))
-
-        def load_w1(e, h):
-            w1_raw[e, h] = ring.tile([P, PACK, HALF], F32, name="w1_raw", bufs=2 * E)
-            nc.sync.dma_start(
-                w1_raw[e, h][:], w1[e][:, h * HALF : (h + 1) * HALF].rearrange("(p j) k -> p j k", j=PACK)
-            )
+        for item in LOADS.split():
+            if item == "d":
+                nc.sync.dma_start(dy_w[:], dy_words[0].rearrange("p t d -> p (t d)").bitcast(I32))
+            elif item == "g":
+                nc.sync.dma_start(gate_rows[0 : S // P, :], gate[0].rearrange("(c s) -> c s", s=P))
+                gate_t = psum.tile([P, PACK, P], F32, name="turned", tag="turned", bufs=4)
+                nc.tensor.transpose(gate_t[:, 0, :], gate_rows[:], ident[:])
+                nc.scalar.activation(gate2[:], gate_t[:, 0, 0 : S // P], COPY, scale=2.0)
+            elif item[0] == "w":
+                e = int(item[1])
+                w2_raw[e] = place("w2_raw%d" % e, [P, PACK, H], F32, W_ROWS + e * 8192)
+                nc.sync.dma_start(w2_raw[e][:], w2[e].rearrange("(p j) i -> p j i", j=PACK))
+            elif item[0] in ("a", "b", "c"):
+                e = int(item[1])
+                lo, hi = {"a": (0, C), "b": (0, C // 2), "c": (C // 2, C)}[item[0]]
+                rows = place("a_" + item, [P, PACK, hi - lo], F32, A_ROWS + e * 8192 + lo * 16)
+                nc.sync.dma_start(rows[:], a[:, e * C + lo : e * C + hi].rearrange("(p j) s -> p j s", j=PACK))
+                for c in range(lo // P, hi // P):
+                    a_sb[e, c] = rows[:, :, c * P - lo : (c + 1) * P - lo]
+            else:
+                e = int(item[1])
+                lo, hi = {"q": (0, P), "r": (P, 2 * P), "n": (0, 2 * P), "f": (2 * P, K)}[item[0]]
+                raw = keep.tile([P, PACK, hi - lo], F32, name="w1_raw_" + item)
+                nc.sync.dma_start(raw[:], w1[e][:, lo:hi].rearrange("(p j) k -> p j k", j=PACK))
+                for kb in range(lo // P, hi // P):
+                    w1_raw[e, kb] = raw[:, :, kb * P - lo : (kb + 1) * P - lo]
 
         def interleave(copy, dst, src):
             copy(dst.rearrange("p (c i) j -> p c j i", i=2), src.rearrange("p j (c i) -> p c j i", i=2))
 
-        def quantize(name, grouped, width, fmt, bufs, parts=1):
-            codes = ring.tile([P, width], U32, name=name + "_codes", bufs=bufs, align_bytes=64)
-            scales = ring.tile([P, width], U8, name=name + "_scales", bufs=bufs, align_bytes=64)
-            for h in range(parts):
-                cols = slice(h * width // parts, (h + 1) * width // parts)
-                nc.vector.quantize_mx(
-                    out=codes[:, cols].bitcast(fmt),
-                    scales=scales[:, cols],
-                    in_=grouped[:, cols, :].rearrange("p c j -> p (c j)"),
-                )
-            return codes, scales
+        def quantize(codes, scales, rounded, fmt):
+            nc.vector.quantize_mx(out=codes.bitcast(fmt), scales=scales, in_=rounded.rearrange("p c j -> p (c j)"))
 
-        def gather(name, window, dtype, e):
-            got = ring.tile([P, C], dtype, name=name, bufs=E, align_bytes=64)
+        def gather(got, window, e):
             nc.vector.tensor_copy(got[:], window.indirect(offs_sb[:, e * C // 16 : (e + 1) * C // 16]))
             return got
 
-        def prepare_w2(e):
-            grouped = ring.tile([P, H, PACK], BF16, name="w2_bf", tag="grouped", bufs=E - 1, align_bytes=64)
+        def gather_words(e, offset):
+            g_words[e] = gather(place("g_words%d" % e, [P, C], U32, offset), dy_w[:].bitcast(U32), e)
+
+        def prepare_w2(e, rounded_at, codes_at):
+            rounded = place("w2_bf%d" % e, [P, H, PACK], BF16, rounded_at)
             for h in range(2):
                 cols = slice(h * H // 2, (h + 1) * H // 2)
-                if e >= E - W2G:
-                    src = w2_raw[e][:, :, cols].rearrange("p j k -> p k j")
-                    nc.gpsimd.tensor_scalar(grouped[:, cols, :], src, 1.0, 0.0, ALU.mult, ALU.add)
-                else:
-                    copy = nc.vector.tensor_copy if e >= E - W2V else nc.scalar.copy
-                    interleave(copy, grouped[:, cols, :], w2_raw[e][:, :, cols])
-            w2_mx[e] = quantize("wide", grouped, H, E4M3, E)
+                interleave(nc.scalar.copy, rounded[:, cols, :], w2_raw[e][:, :, cols])
+            codes = place("w2_codes%d" % e, [P, H], U32, codes_at)
+            scales = place("w2_scales%d" % e, [P, H], U8, period(e + 1) if e + 1 < E else W_ROWS + E * 8192 + 512)
+            quantize(codes[:], scales[:], rounded[:], E4M3)
+            w2_mx[e] = codes, scales
+
+        def prepare_w1(experts, kb, copy, rounded_at, codes_at):
+            width = len(experts) * P
+            name = "w1_%d_%d" % (kb, experts[0])
+            rounded = place(name + "_bf", [P, width, PACK], BF16, rounded_at)
+            for n, e in enumerate(experts):
+                interleave(copy, rounded[:, n * P : (n + 1) * P, :], w1_raw[e, kb])
+            codes = place(name + "_codes", [P, width], U32, codes_at)
+            scales = keep.tile([P, width], U8, name=name + "_scales", align_bytes=64)
+            quantize(codes[:], scales[:], rounded[:], E4M3)
+            for n, e in enumerate(experts):
+                w1_mx[e, kb] = codes[:, n * P : (n + 1) * P], scales[:, n * P : (n + 1) * P]
+
+        def quantize_da(e):
+            codes = place("da_codes%d" % e, [P, C], U32, A_ROWS + e * 8192)
+            scales = place("da_scales%d" % e, [P, C], U8, A_ROWS + e * 8192 + 2048)
+            quantize(codes[:], scales[:], da[e][:], E5M2)
+            da_mx[e] = codes, scales
 
         def first_layer(e):
-            words, scales = dy_mx[e]
-            da = ring.tile([P, C, PACK], BF16, name="da", tag="da", bufs=2, align_bytes=64)
+            da[e] = place("da%d" % e, [P, C, PACK], BF16, period(e) + DA)
+            sums = [psum.tile([P, H], F32, name="sums", tag="sums", bufs=4) for c in range(CHUNKS)]
             for c in range(CHUNKS):
                 cols = slice(c * P, (c + 1) * P)
-                sums = psum.tile([P, H], F32, name="sums", tag="sums", bufs=SUMS)
                 nc.tensor.matmul_mx(
-                    out=sums[:],
-                    lhsT=words[:, cols].bitcast(E5M2),
-                    lhsT_scale=scales[:, cols],
+                    out=sums[c][:],
+                    lhsT=g_words[e][:, cols].bitcast(E5M2),
+                    lhsT_scale=g_scales[e][:, cols],
                     rhs=w2_mx[e][0][:].bitcast(E4M3),
                     rhs_scale=w2_mx[e][1][:],
                     start=True,
                     stop=True,
                 )
-                dh = ring.tile([P, PACK, P], F32, name="dh", bufs=DH, align_bytes=64)
+            for c in range(CHUNKS):
+                cols = slice(c * P, (c + 1) * P)
+                dh = keep.tile([P, PACK, P], F32, name="dh", bufs=8, align_bytes=64)[:]
                 col = e * CHUNKS + c
                 nc.scalar.activation(
-                    dh[:], sums[:].rearrange("s (p j) -> s j p", j=PACK), COPY, scale=gate2[:, col : col + 1]
+                    dh, sums[c][:].rearrange("s (p j) -> s j p", j=PACK), COPY, scale=gate2[:, col : col + 1]
                 )
-                turned = psum.tile([P, PACK, P], F32, name="turned", tag="turned", bufs=TURN)
+                turned = psum.tile([P, PACK, P], F32, name="turned", tag="turned", bufs=4)
                 for j in range(PACK):
                     nc.tensor.transpose(turned[:, j, :], dh[:, j, :], ident[:])
-                if c == POS and 0 < e <= NOW:
-                    second_layer(e - 1, 0, "turned", TURN)
-                if e >= R0 and c >= CHUNKS - RC:
-                    slope = ring.tile([P, P, PACK], F32, name="slope", bufs=RC, align_bytes=64)
-                    nc.scalar.activation(
-                        slope[:].rearrange("p (c i) j -> p c j i", i=2),
-                        a_sb[e][:, :, cols].rearrange("p j (c i) -> p c j i", i=2),
-                        RELU,
+                if c >= HOP + (e == E - 1) * 1:
+                    slope = place("slope%d%d" % (e, c), [P, PACK, P], F32, period(e - 1) + SLOPE + (c - 1) * 2048)
+                    nc.gpsimd.tensor_scalar(slope[:], a_sb[e, c], FLOAT_MAX, 0.0, ALU.min, ALU.max)
+                    nc.vector.tensor_tensor(
+                        da[e][:, cols, :].rearrange("p (c i) j -> p c j i", i=2),
+                        turned[:].rearrange("p j (c i) -> p c j i", i=2),
+                        slope[:].rearrange("p j (c i) -> p c j i", i=2),
+                        ALU.mult,
                     )
-                    nc.vector.tensor_tensor(da[:, cols, :], turned[:].rearrange("p j s -> p s j"), slope[:], ALU.mult)
                 else:
                     nc.vector.scalar_tensor_tensor(
-                        out=da[:, cols, :],
-                        in0=a_sb[e][:, :, cols].rearrange("p j s -> p s j"),
+                        out=da[e][:, cols, :],
+                        in0=a_sb[e, c].rearrange("p j s -> p s j"),
                         scalar=0.0,
                         in1=turned[:].rearrange("p j s -> p s j"),
                         op0=ALU.max,
                         op1=ALU.mult,
                     )
-            da_mx[e] = quantize("da", da, C, E5M2, E, 2)
 
-        def prepare_w1(experts, kb, copy=nc.scalar.copy):
-            tag, name, bufs = {1: ("w1_bf", "narrow", E), 2: ("da", "pair", 2), 4: ("grouped", "wide", E - 1)}[len(experts)]
-            grouped = ring.tile([P, len(experts) * P, PACK], BF16, name="w1_bf", tag=tag, bufs=bufs, align_bytes=64)
-            for n, e in enumerate(experts):
-                interleave(
-                    copy,
-                    grouped[:, n * P : (n + 1) * P, :],
-                    w1_raw[e, kb // 2][:, :, kb % 2 * P : (kb % 2 + 1) * P],
-                )
-            codes, scales = quantize(name, grouped, len(experts) * P, E4M3, 2 if name == "pair" else E)
-            for n, e in enumerate(experts):
-                w1_mx[e, kb] = codes[:, n * P : (n + 1) * P], scales[:, n * P : (n + 1) * P]
-
-        def prepare_w1_block(kb):
-            prepare_w1(list(range(E - 1)), kb)
-            prepare_w1([E - 1], kb)
-
-        def second_layer(e, kb, tag="sums", bufs=SUMS):
+        def second_layer(e, kb, acc=None):
             codes, scales = w1_mx[e, kb]
-            acc = psum.tile([P, C], F32, name="acc", tag=tag, bufs=bufs)
+            if acc is None:
+                acc = psum.tile([P, C], F32, name="acc", tag="turned", bufs=4)[:]
             nc.tensor.matmul_mx(
-                out=acc[:],
+                out=acc,
                 lhsT=codes.bitcast(E4M3),
                 lhsT_scale=scales,
                 rhs=da_mx[e][0][:].bitcast(E5M2),
@@ -189,54 +195,56 @@ def tile_moe_bdx_mlp_relu2_kernel(
                 start=True,
                 stop=True,
             )
-            nc.scalar.copy(dx[kb][:, e * C : (e + 1) * C], acc[:])
+            nc.scalar.copy(dx[kb][:, e * C : (e + 1) * C], acc)
+
+        def staging(n):
+            return A_ROWS + n % 10 // 2 * 8192 + 2560 + n % 2 * 2560
 
         def combine(kb):
-            cuts = [0, T // 2, T] if kb + 1 < K // P else [0, T // 2, T - 256, T - 128, T]
+            cuts = [0, T // 2, T] if kb + 1 < BLOCKS else [0, T // 2, T - 256, T - 128, T]
             firsts = []
-            for lo in (0, T // 2):
-                first = ring.tile([P, T // 2], F32, name="first", bufs=3)
-                nc.vector.tensor_copy(first[:], dx[kb][:].indirect(pos1_sb[:, lo // 16 : (lo + T // 2) // 16]))
+            for h in range(2):
+                first = place("first%d%d" % (kb, h), [P, T // 2], F32, staging(4 * kb + h))
+                nc.vector.tensor_copy(first[:], dx[kb][:].indirect(pos1_sb[:, h * T // 32 : (h + 1) * T // 32]))
                 firsts.append(first)
-            for lo, hi in zip(cuts, cuts[1:]):
+            for n, (lo, hi) in enumerate(zip(cuts, cuts[1:])):
                 first = firsts[lo // (T // 2)][:, lo % (T // 2) : lo % (T // 2) + hi - lo]
-                total = ring.tile([P, hi - lo], F32, name="total", bufs=4)
+                total = place("total%d%d" % (kb, n), [P, hi - lo], F32, staging(4 * kb + 2 + n))
                 nc.vector.tensor_tensor(total[:], dx[kb][:].indirect(pos2_sb[:, lo // 16 : hi // 16]), first, ALU.add)
                 nc.sync.dma_start(out[kb * P : (kb + 1) * P, lo:hi], total[:])
 
-        for item in LOADS.split():
-            if item == "d":
-                nc.sync.dma_start(dy_w[:], dy_words[0].rearrange("p t d -> p (t d)").bitcast(I32))
-            elif item == "g":
-                nc.sync.dma_start(gate_rows[0 : S // P, :], gate[0].rearrange("(c s) -> c s", s=P))
-                gate_t = psum.tile([P, PACK, P], F32, name="turned", tag="turned", bufs=TURN)
-                nc.tensor.transpose(gate_t[:, 0, :], gate_rows[:], ident[:])
-                nc.scalar.activation(gate2[:], gate_t[:, 0, 0 : S // P], COPY, scale=2.0)
-            elif item[0] == "w":
-                load_w2(int(item[1]))
-            elif item[0] == "a":
-                load_a(int(item[1]))
+        for e in range(E - 1):
+            g_scales[e] = gather(keep.tile([P, C], U8, name="g_scales%d" % e, align_bytes=64), dy_s[:], e)
+        gather_words(0, 4096)
+        prepare_w2(0, 0, 6144)
+        gather_words(1, 0)
+        prepare_w2(1, period(-1) + DA, 8192)
+        g_scales[E - 1] = gather(place("g_scales_last", [P, C], U8, W_ROWS + E * 8192), dy_s[:], E - 1)
+        first_layer(0)
+        for e in range(1, E):
+            if e + 1 < E:
+                prepare_w2(e + 1, period(e) + ROUNDED, A_ROWS + e * 8192 - 2048)
             else:
-                load_w1(int(item[1]), 0 if item[0] == "n" else 1)
-        g_scales = [gather("g_scales", dy_s[:], U8, e) for e in range(E)]
-        g_words = [gather("g_words", dy_w[:].bitcast(U32), U32, e) for e in range(E)]
-        for e in range(E):
-            dy_mx[e] = g_words[e], g_scales[e]
-            prepare_w2(e)
-        dx = [ring.tile([P, S], F32, name="dx", tag="rows", bufs=E, align_bytes=64) for kb in range(K // P)]
-        for e in range(E):
+                prepare_w1(list(range(E - 1)), 0, nc.scalar.copy, period(e) + ROUNDED, A_ROWS + e * 8192 - 2048)
+            quantize_da(e - 1)
+            if e + 1 < E:
+                gather_words(e + 1, period(e) + WORDS)
             first_layer(e)
-            prepare_w1([e], 0)
-        for e in range(NOW, E - 1):
-            second_layer(e, 0)
-        prepare_w1([2], 1)
-        prepare_w1([0, 1], 1)
-        prepare_w1([3, 4], 1, nc.vector.tensor_copy)
-        second_layer(E - 1, 0, "turned", TURN)
-        for kb in range(K // P):
-            if kb + 2 < K // P:
-                prepare_w1_block(kb + 2)
+        dx = [place("dx%d" % kb, [P, S], F32, W_ROWS + kb * 10240) for kb in range(BLOCKS)]
+        prepare_w1([E - 1], 0, nc.scalar.copy, 1024, A_ROWS + E * 8192 - 512)
+        quantize_da(E - 1)
+        for e in range(E - 1):
+            second_layer(e, 0, psum.tile([P, C], F32, name="waiting", tag="sums", bufs=4)[:])
+        second_layer(E - 1, 0)
+        prepare_w1([3, 4], 1, nc.vector.tensor_copy, 1984, 6144)
+        prepare_w1([0, 1], 1, nc.scalar.copy, A_ROWS + 3 * 8192 - 2048, 64)
+        prepare_w1([2], 1, nc.scalar.copy, A_ROWS + 3 * 8192 - 3008, 1152)
+        for kb in range(BLOCKS):
+            if kb + 2 < BLOCKS:
+                base = (A_ROWS + E * 8192 - 4544, 7104)[kb]
+                prepare_w1(list(range(E - 1)), kb + 2, nc.scalar.copy, base, period(kb))
+                prepare_w1([E - 1], kb + 2, nc.scalar.copy, period(2) if kb == 0 else 5184, period(kb) + 2048)
             combine(kb)
-            if kb + 1 < K // P:
+            if kb + 1 < BLOCKS:
                 for e in range(E):
                     second_layer(e, kb + 1)

@@ -23,15 +23,18 @@ P = 128
 PACK = 4
 CHUNKS = C // P
 BLOCKS = K // P
-HOP = 1
 FLOAT_MAX = 3.4028234663852886e38
-LOADS = "w0 w1 d g b0 w2 c0 w3 a1 w4 a2 q0 q1 q2 q3 a3 a4 q4 r0 r1 r2 r3 r4 f0 f1 f2 f3 f4"
+LOADS = "w0 w1 d g w2 a0 w3 a1 w4 a2 q0 q1 a3 q2 q3 a4 q4 r2 r3 r4 r0 r1 f0 f1 f2 f3 f4"
 
 HEAD = 10240
 PERIOD = 8192
-ROUNDED, WORDS, SLOPE, DA, CODES = 0, 0, 2048, 3584, 4096
+ROUNDED, WORDS, SLOPE, DA = 0, 0, 2048, 3584
+BANKS = (1, 2, 2, 2, 2, 2)
+HOPS = (1,1,1,2,2)
 A_ROWS = HEAD + (E + 1) * PERIOD
 W_ROWS = A_ROWS + E * 8192
+W1_ROWS = W_ROWS + E * 8192 + 1024
+PAIR = W1_ROWS + E * 8192 + 512
 
 
 def tile_moe_bdx_mlp_relu2_kernel(
@@ -43,9 +46,15 @@ def tile_moe_bdx_mlp_relu2_kernel(
         keep = ctx.enter_context(tc.tile_pool(name="keep", bufs=1))
         laid = ctx.enter_context(tc.tile_pool(name="laid", bufs=1))
         psum = ctx.enter_context(tc.psum_pool(name="psum", bufs=1))
+        banks = ctx.enter_context(tc.psum_pool(name="banks", bufs=1))
 
         def place(name, shape, dtype, offset):
             return laid.tile(shape, dtype, name=name, offset=offset, align_bytes=64)
+
+        def four_banks(turn):
+            n = BANKS[turn]
+            tiles = [banks.tile([P, n, H], F32, name="sums%d%d" % (turn, b), offset=b * 2048) for b in range(0, 4, n)]
+            return [tiles[b // n][:, b % n, :] for b in range(4)]
 
         def period(e):
             return HEAD + (e + 1) * PERIOD
@@ -69,8 +78,10 @@ def tile_moe_bdx_mlp_relu2_kernel(
         nc.sync.dma_start(pos2_sb[:], pos2)
 
         w2_raw, a_sb, w1_raw = {}, {}, {}
+        turned, w1_far = {}, {}
         w2_mx, g_words, g_scales, da, da_mx, w1_mx = {}, {}, {}, {}, {}, {}
 
+        w1_pair = place("w1_pair", [P, 2, PACK, P], F32, PAIR)
         for item in LOADS.split():
             if item == "d":
                 nc.sync.dma_start(dy_w[:], dy_words[0].rearrange("p t d -> p (t d)").bitcast(I32))
@@ -92,9 +103,13 @@ def tile_moe_bdx_mlp_relu2_kernel(
                     a_sb[e, c] = rows[:, :, c * P - lo : (c + 1) * P - lo]
             else:
                 e = int(item[1])
-                lo, hi = {"q": (0, P), "r": (P, 2 * P), "n": (0, 2 * P), "f": (2 * P, K)}[item[0]]
-                raw = keep.tile([P, PACK, hi - lo], F32, name="w1_raw_" + item)
-                nc.sync.dma_start(raw[:], w1[e][:, lo:hi].rearrange("(p j) k -> p j k", j=PACK))
+                lo, hi = {"q": (0, P), "r": (P, 2 * P), "n": (0, 2 * P), "f": (2 * P, K), "t": (P, K)}[item[0]]
+                if item in ("r0", "r1"):
+                    raw = w1_pair[:, e]
+                else:
+                    raw = place("w1_raw_" + item, [P, PACK, hi - lo], F32, W1_ROWS + e * 8192 + lo * 16)[:]
+                w1_far[e] = raw
+                nc.sync.dma_start(raw, w1[e][:, lo:hi].rearrange("(p j) k -> p j k", j=PACK))
                 for kb in range(lo // P, hi // P):
                     w1_raw[e, kb] = raw[:, :, kb * P - lo : (kb + 1) * P - lo]
 
@@ -121,17 +136,38 @@ def tile_moe_bdx_mlp_relu2_kernel(
             quantize(codes[:], scales[:], rounded[:], E4M3)
             w2_mx[e] = codes, scales
 
-        def prepare_w1(experts, kb, copy, rounded_at, codes_at):
-            width = len(experts) * P
-            name = "w1_%d_%d" % (kb, experts[0])
-            rounded = place(name + "_bf", [P, width, PACK], BF16, rounded_at)
+        def round_w1(experts, kb, copy, rounded_at):
+            rounded = place("w1_%d_%d_bf" % (kb, experts[0]), [P, len(experts) * P, PACK], BF16, rounded_at)
             for n, e in enumerate(experts):
                 interleave(copy, rounded[:, n * P : (n + 1) * P, :], w1_raw[e, kb])
+            return rounded
+
+        def prepare_w1(experts, kb, copy, rounded_at, codes_at):
+            quantize_w1(experts, kb, round_w1(experts, kb, copy, rounded_at), codes_at)
+
+        def quantize_w1(experts, kb, rounded, codes_at, scales_at=None):
+            width = len(experts) * P
+            name = "w1_%d_%d" % (kb, experts[0])
             codes = place(name + "_codes", [P, width], U32, codes_at)
-            scales = keep.tile([P, width], U8, name=name + "_scales", align_bytes=64)
+            if scales_at is None:
+                scales = keep.tile([P, width], U8, name=name + "_scales", align_bytes=64)
+            else:
+                scales = place(name + "_scales", [P, width], U8, scales_at)
             quantize(codes[:], scales[:], rounded[:], E4M3)
             for n, e in enumerate(experts):
                 w1_mx[e, kb] = codes[:, n * P : (n + 1) * P], scales[:, n * P : (n + 1) * P]
+
+        def prepare_far(experts, rounded_at, codes_at):
+            width = len(experts) * 2 * P
+            name = "w1_far%d" % experts[0]
+            rounded = place(name + "_bf", [P, width, PACK], BF16, rounded_at)
+            for n, e in enumerate(experts):
+                interleave(nc.scalar.copy, rounded[:, n * 2 * P : (n + 1) * 2 * P, :], w1_far[e])
+            codes = place(name + "_codes", [P, width], U32, codes_at)
+            scales = keep.tile([P, width], U8, name=name + "_scales", align_bytes=64)
+            quantize(codes[:], scales[:], rounded[:], E4M3)
+            for n in range(width // P):
+                w1_mx[experts[n // 2], 2 + n % 2] = codes[:, n * P : (n + 1) * P], scales[:, n * P : (n + 1) * P]
 
         def quantize_da(e):
             codes = place("da_codes%d" % e, [P, C], U32, A_ROWS + e * 8192)
@@ -139,13 +175,12 @@ def tile_moe_bdx_mlp_relu2_kernel(
             quantize(codes[:], scales[:], da[e][:], E5M2)
             da_mx[e] = codes, scales
 
-        def first_layer(e):
-            da[e] = place("da%d" % e, [P, C, PACK], BF16, period(e) + DA)
-            sums = [psum.tile([P, H], F32, name="sums", tag="sums", bufs=4) for c in range(CHUNKS)]
+        def front(e):
+            sums = four_banks(e)
             for c in range(CHUNKS):
                 cols = slice(c * P, (c + 1) * P)
                 nc.tensor.matmul_mx(
-                    out=sums[c][:],
+                    out=sums[c],
                     lhsT=g_words[e][:, cols].bitcast(E5M2),
                     lhsT_scale=g_scales[e][:, cols],
                     rhs=w2_mx[e][0][:].bitcast(E4M3),
@@ -154,38 +189,45 @@ def tile_moe_bdx_mlp_relu2_kernel(
                     stop=True,
                 )
             for c in range(CHUNKS):
-                cols = slice(c * P, (c + 1) * P)
-                dh = keep.tile([P, PACK, P], F32, name="dh", bufs=8, align_bytes=64)[:]
+                dh = keep.tile([P, PACK, P], F32, name="dh", bufs=8, align_bytes=64)
                 col = e * CHUNKS + c
                 nc.scalar.activation(
-                    dh, sums[c][:].rearrange("s (p j) -> s j p", j=PACK), COPY, scale=gate2[:, col : col + 1]
+                    dh[:], sums[c].rearrange("s (p j) -> s j p", j=PACK), COPY, scale=gate2[:, col : col + 1]
                 )
-                turned = psum.tile([P, PACK, P], F32, name="turned", tag="turned", bufs=4)
+                turned[e, c] = psum.tile([P, PACK, P], F32, name="turned", tag="turned", bufs=4)
                 for j in range(PACK):
-                    nc.tensor.transpose(turned[:, j, :], dh[:, j, :], ident[:])
-                if c >= HOP + (e == E - 1) * 1:
-                    slope = place("slope%d%d" % (e, c), [P, PACK, P], F32, period(e - 1) + SLOPE + (c - 1) * 2048)
-                    nc.gpsimd.tensor_scalar(slope[:], a_sb[e, c], FLOAT_MAX, 0.0, ALU.min, ALU.max)
-                    nc.vector.tensor_tensor(
-                        da[e][:, cols, :].rearrange("p (c i) j -> p c j i", i=2),
-                        turned[:].rearrange("p j (c i) -> p c j i", i=2),
-                        slope[:].rearrange("p j (c i) -> p c j i", i=2),
-                        ALU.mult,
-                    )
-                else:
-                    nc.vector.scalar_tensor_tensor(
-                        out=da[e][:, cols, :],
-                        in0=a_sb[e, c].rearrange("p j s -> p s j"),
-                        scalar=0.0,
-                        in1=turned[:].rearrange("p j s -> p s j"),
-                        op0=ALU.max,
-                        op1=ALU.mult,
-                    )
+                    nc.tensor.transpose(turned[e, c][:, j, :], dh[:, j, :], ident[:])
 
-        def second_layer(e, kb, acc=None):
+        def product(e, c):
+            if c == 0:
+                da[e] = place("da%d" % e, [P, C, PACK], BF16, period(e) + DA)
+            cols = slice(c * P, (c + 1) * P)
+            if c >= HOPS[e]:
+                slope = place("slope%d%d" % (e, c), [P, PACK, P], F32, period(e - 1) + SLOPE + (c - 1) * 2048)
+                nc.gpsimd.tensor_scalar(slope[:], a_sb[e, c], FLOAT_MAX, 0.0, ALU.min, ALU.max)
+                nc.vector.tensor_tensor(
+                    da[e][:, cols, :].rearrange("p (c i) j -> p c j i", i=2),
+                    slope[:].rearrange("p j (c i) -> p c j i", i=2),
+                    turned[e, c][:].rearrange("p j (c i) -> p c j i", i=2),
+                    ALU.mult,
+                )
+            else:
+                nc.vector.scalar_tensor_tensor(
+                    out=da[e][:, cols, :],
+                    in0=a_sb[e, c].rearrange("p j s -> p s j"),
+                    scalar=0.0,
+                    in1=turned[e, c][:].rearrange("p j s -> p s j"),
+                    op0=ALU.max,
+                    op1=ALU.mult,
+                )
+
+        def second_layer(e, kb):
+            acc = psum.tile([P, C], F32, name="acc", tag="turned", bufs=4)[:]
+            second_matmul(e, kb, acc)
+            nc.scalar.copy(dx[kb][:, e * C : (e + 1) * C], acc)
+
+        def second_matmul(e, kb, acc):
             codes, scales = w1_mx[e, kb]
-            if acc is None:
-                acc = psum.tile([P, C], F32, name="acc", tag="turned", bufs=4)[:]
             nc.tensor.matmul_mx(
                 out=acc,
                 lhsT=codes.bitcast(E4M3),
@@ -195,21 +237,22 @@ def tile_moe_bdx_mlp_relu2_kernel(
                 start=True,
                 stop=True,
             )
-            nc.scalar.copy(dx[kb][:, e * C : (e + 1) * C], acc)
 
         def staging(n):
             return A_ROWS + n % 10 // 2 * 8192 + 2560 + n % 2 * 2560
+
+        held = {(0, 1): PAIR - 512, (0, 2): PAIR + 2048, (1, 1): W1_ROWS + 8192 + 4096, (1, 2): W1_ROWS + 3 * 8192 + 4096, (1, 3): W1_ROWS + 4 * 8192 + 4096}
 
         def combine(kb):
             cuts = [0, T // 2, T] if kb + 1 < BLOCKS else [0, T // 2, T - 256, T - 128, T]
             firsts = []
             for h in range(2):
-                first = place("first%d%d" % (kb, h), [P, T // 2], F32, staging(4 * kb + h))
+                first = place("first%d%d" % (kb, h), [P, T // 2], F32, held.get((kb, h), staging(4 * kb + h)))
                 nc.vector.tensor_copy(first[:], dx[kb][:].indirect(pos1_sb[:, h * T // 32 : (h + 1) * T // 32]))
                 firsts.append(first)
             for n, (lo, hi) in enumerate(zip(cuts, cuts[1:])):
                 first = firsts[lo // (T // 2)][:, lo % (T // 2) : lo % (T // 2) + hi - lo]
-                total = place("total%d%d" % (kb, n), [P, hi - lo], F32, staging(4 * kb + 2 + n))
+                total = place("total%d%d" % (kb, n), [P, hi - lo], F32, held.get((kb, 2 + n), staging(4 * kb + 2 + n)))
                 nc.vector.tensor_tensor(total[:], dx[kb][:].indirect(pos2_sb[:, lo // 16 : hi // 16]), first, ALU.add)
                 nc.sync.dma_start(out[kb * P : (kb + 1) * P, lo:hi], total[:])
 
@@ -220,31 +263,41 @@ def tile_moe_bdx_mlp_relu2_kernel(
         gather_words(1, 0)
         prepare_w2(1, period(-1) + DA, 8192)
         g_scales[E - 1] = gather(place("g_scales_last", [P, C], U8, W_ROWS + E * 8192), dy_s[:], E - 1)
-        first_layer(0)
+        gather_words(2, W_ROWS + 8192)
+        front(0)
+        for c in range(CHUNKS):
+            product(0, c)
         for e in range(1, E):
             if e + 1 < E:
                 prepare_w2(e + 1, period(e) + ROUNDED, A_ROWS + e * 8192 - 2048)
             else:
                 prepare_w1(list(range(E - 1)), 0, nc.scalar.copy, period(e) + ROUNDED, A_ROWS + e * 8192 - 2048)
+            front(e)
             quantize_da(e - 1)
-            if e + 1 < E:
-                gather_words(e + 1, period(e) + WORDS)
-            first_layer(e)
+            if e + 2 < E:
+                gather_words(e + 2, period(e) + WORDS)
+            for c in range(CHUNKS):
+                product(e, c)
         dx = [place("dx%d" % kb, [P, S], F32, W_ROWS + kb * 10240) for kb in range(BLOCKS)]
         prepare_w1([E - 1], 0, nc.scalar.copy, 1024, A_ROWS + E * 8192 - 512)
         quantize_da(E - 1)
+        waiting = four_banks(E)
         for e in range(E - 1):
-            second_layer(e, 0, psum.tile([P, C], F32, name="waiting", tag="sums", bufs=4)[:])
+            second_matmul(e, 0, waiting[e])
+        for e in range(E - 1):
+            nc.scalar.copy(dx[0][:, e * C : (e + 1) * C], waiting[e])
         second_layer(E - 1, 0)
+        prepare_w1([2], 1, nc.vector.tensor_copy, 64, 8192)
         prepare_w1([3, 4], 1, nc.vector.tensor_copy, 1984, 6144)
-        prepare_w1([0, 1], 1, nc.scalar.copy, A_ROWS + 3 * 8192 - 2048, 64)
-        prepare_w1([2], 1, nc.scalar.copy, A_ROWS + 3 * 8192 - 3008, 1152)
-        for kb in range(BLOCKS):
-            if kb + 2 < BLOCKS:
-                base = (A_ROWS + E * 8192 - 4544, 7104)[kb]
-                prepare_w1(list(range(E - 1)), kb + 2, nc.scalar.copy, base, period(kb))
-                prepare_w1([E - 1], kb + 2, nc.scalar.copy, period(2) if kb == 0 else 5184, period(kb) + 2048)
+        prepare_w1([0, 1], 1, nc.scalar.copy, A_ROWS + 4 * 8192 - 2048, period(3))
+        for e in range(E):
+            second_layer(e, 1)
+        combine(0)
+        prepare_far([0, 1], A_ROWS + E * 8192 - 4544, period(1))
+        prepare_far([2, 3], W1_ROWS + 4096, period(1) + 2048)
+        prepare_far([4], W1_ROWS + 2 * 8192 + 4096, period(1) + 4096)
+        combine(1)
+        for kb in range(2, BLOCKS):
+            for e in range(E):
+                second_layer(e, kb)
             combine(kb)
-            if kb + 1 < BLOCKS:
-                for e in range(E):
-                    second_layer(e, kb + 1)

@@ -24,13 +24,13 @@ PACK = 4
 CHUNKS = C // P
 BLOCKS = K // P
 FLOAT_MAX = 3.4028234663852886e38
-LOADS = "w0 w1 d g w2 a0 w3 a1 w4 a2 q0 q1 a3 q2 q3 a4 q4 r2 r3 r4 r0 r1 f0 f1 f2 f3 f4"
+LOADS = "w0 w1 d g w2 a0 w3 a1 w4 a2 a3 q0 q1 a4 q2 q3 q4 r2 r3 r4 r0 r1 f0 f1 f2 f3 f4"
 
 HEAD = 10240
 PERIOD = 8192
 ROUNDED, WORDS, SLOPE, DA = 0, 0, 2048, 3584
-BANKS = (1, 2, 2, 2, 2, 2)
-HOPS = (1,1,1,2,2)
+BANKS = (1, 2, 2, 2, 2, 1)
+HOPS = (1, 1, 1, 2, 2)
 A_ROWS = HEAD + (E + 1) * PERIOD
 W_ROWS = A_ROWS + E * 8192
 W1_ROWS = W_ROWS + E * 8192 + 1024
@@ -132,7 +132,7 @@ def tile_moe_bdx_mlp_relu2_kernel(
                 cols = slice(h * H // 2, (h + 1) * H // 2)
                 interleave(nc.scalar.copy, rounded[:, cols, :], w2_raw[e][:, :, cols])
             codes = place("w2_codes%d" % e, [P, H], U32, codes_at)
-            scales = place("w2_scales%d" % e, [P, H], U8, period(e + 1) if e + 1 < E else W_ROWS + E * 8192 + 512)
+            scales = place("w2_scales%d" % e, [P, H], U8, period(e + 1) + 2048 if e + 1 < E else W_ROWS + E * 8192 + 512)
             quantize(codes[:], scales[:], rounded[:], E4M3)
             w2_mx[e] = codes, scales
 
@@ -189,7 +189,10 @@ def tile_moe_bdx_mlp_relu2_kernel(
                     stop=True,
                 )
             for c in range(CHUNKS):
-                dh = keep.tile([P, PACK, P], F32, name="dh", bufs=8, align_bytes=64)
+                if e + 1 == E and c < 2:
+                    dh = place("dh_last%d" % c, [P, PACK, P], F32, W1_ROWS + c * 8192)
+                else:
+                    dh = keep.tile([P, PACK, P], F32, name="dh", bufs=6, align_bytes=64)
                 col = e * CHUNKS + c
                 nc.scalar.activation(
                     dh[:], sums[c].rearrange("s (p j) -> s j p", j=PACK), COPY, scale=gate2[:, col : col + 1]
@@ -271,7 +274,7 @@ def tile_moe_bdx_mlp_relu2_kernel(
             if e + 1 < E:
                 prepare_w2(e + 1, period(e) + ROUNDED, A_ROWS + e * 8192 - 2048)
             else:
-                prepare_w1(list(range(E - 1)), 0, nc.scalar.copy, period(e) + ROUNDED, A_ROWS + e * 8192 - 2048)
+                prepare_w1([0, 1], 0, nc.scalar.copy, period(e) + 2048, A_ROWS + e * 8192 - 2048)
             front(e)
             quantize_da(e - 1)
             if e + 2 < E:
@@ -279,21 +282,30 @@ def tile_moe_bdx_mlp_relu2_kernel(
             for c in range(CHUNKS):
                 product(e, c)
         dx = [place("dx%d" % kb, [P, S], F32, W_ROWS + kb * 10240) for kb in range(BLOCKS)]
-        prepare_w1([E - 1], 0, nc.scalar.copy, 1024, A_ROWS + E * 8192 - 512)
+        last = A_ROWS + E * 8192
+        spent = A_ROWS + 3 * 8192 - 2048
+        prepare_w1([2, 3], 0, nc.scalar.copy, spent, last - 1024)
         quantize_da(E - 1)
+        rounded4 = round_w1([4], 0, nc.vector.tensor_copy, spent + 512)
+        single = round_w1([2], 1, nc.vector.tensor_copy, spent - 960)
+        quantize_w1([4], 0, rounded4, last - 1536)
         waiting = four_banks(E)
+        waiting = waiting[2:] + waiting[:2]
         for e in range(E - 1):
             second_matmul(e, 0, waiting[e])
+        acc = psum.tile([P, C], F32, name="acc", tag="turned", bufs=4)[:]
+        second_matmul(E - 1, 0, acc)
         for e in range(E - 1):
             nc.scalar.copy(dx[0][:, e * C : (e + 1) * C], waiting[e])
-        second_layer(E - 1, 0)
-        prepare_w1([2], 1, nc.vector.tensor_copy, 64, 8192)
-        prepare_w1([3, 4], 1, nc.vector.tensor_copy, 1984, 6144)
-        prepare_w1([0, 1], 1, nc.scalar.copy, A_ROWS + 4 * 8192 - 2048, period(3))
+        nc.scalar.copy(dx[0][:, (E - 1) * C :], acc)
+        pair = round_w1([3, 4], 1, nc.vector.tensor_copy, spent - 2944)
+        quantize_w1([2], 1, single, 8192)
+        quantize_w1([3, 4], 1, pair, 6144)
+        prepare_w1([0, 1], 1, nc.scalar.copy, last - 3008, period(3))
         for e in range(E):
             second_layer(e, 1)
         combine(0)
-        prepare_far([0, 1], A_ROWS + E * 8192 - 4544, period(1))
+        prepare_far([0, 1], 7104, period(1))
         prepare_far([2, 3], W1_ROWS + 4096, period(1) + 2048)
         prepare_far([4], W1_ROWS + 2 * 8192 + 4096, period(1) + 4096)
         combine(1)

@@ -23,18 +23,18 @@ P = 128
 PACK = 4
 CHUNKS = C // P
 BLOCKS = K // P
+HALF = T // 2
 FLOAT_MAX = 3.4028234663852886e38
-LOADS = "w0 w1 d g w2 a0 w3 a1 w4 a2 a3 q0 q1 a4 q2 q3 q4 r2 r3 r4 r0 r1 f0 f1 f2 f3 f4"
+FUSED = (0, 0, 2, 2, 2)
 
-HEAD = 10240
-PERIOD = 8192
-ROUNDED, WORDS, SLOPE, DA = 0, 0, 2048, 3584
-BANKS = (1, 2, 2, 2, 2, 1)
-HOPS = (1, 1, 1, 2, 2)
-A_ROWS = HEAD + (E + 1) * PERIOD
-W_ROWS = A_ROWS + E * 8192
-W1_ROWS = W_ROWS + E * 8192 + 1024
-PAIR = W1_ROWS + E * 8192 + 512
+MATRIX = 8192
+QUARTER = MATRIX // 4
+W2_AT = 0
+A_AT = W2_AT + E * MATRIX
+W1_AT = A_AT + E * MATRIX
+FIRST_AT = W1_AT + E * MATRIX
+TURN_AT = FIRST_AT + MATRIX
+PAIR_AT = TURN_AT + 3 * MATRIX
 
 
 def tile_moe_bdx_mlp_relu2_kernel(
@@ -46,141 +46,132 @@ def tile_moe_bdx_mlp_relu2_kernel(
         keep = ctx.enter_context(tc.tile_pool(name="keep", bufs=1))
         laid = ctx.enter_context(tc.tile_pool(name="laid", bufs=1))
         psum = ctx.enter_context(tc.psum_pool(name="psum", bufs=1))
-        banks = ctx.enter_context(tc.psum_pool(name="banks", bufs=1))
 
         def place(name, shape, dtype, offset):
+            if offset is None:
+                return keep.tile(shape, dtype, name=name, align_bytes=64)
             return laid.tile(shape, dtype, name=name, offset=offset, align_bytes=64)
 
-        def four_banks(turn):
-            n = BANKS[turn]
-            tiles = [banks.tile([P, n, H], F32, name="sums%d%d" % (turn, b), offset=b * 2048) for b in range(0, 4, n)]
-            return [tiles[b // n][:, b % n, :] for b in range(4)]
+        def turn(e):
+            return TURN_AT + e % 3 * MATRIX
 
-        def period(e):
-            return HEAD + (e + 1) * PERIOD
+        def slopes_at(e):
+            return turn(e - 1) if e else FIRST_AT
 
         offs_sb = lists.tile([P, S // 16], U16, name="offs_sb")
         pos1_sb = lists.tile([P, T // 16], U16, name="pos1_sb")
         pos2_sb = lists.tile([P, T // 16], U16, name="pos2_sb")
-        dy_w = keep.tile([P, T], I32, name="dy_w", align_bytes=64)
-        dy_s = keep.tile([P, T], U8, name="dy_s", align_bytes=64)
-        gate_rows = place("gate_rows", [P, P], F32, W_ROWS + E * 8192)
-        gate2 = keep.tile([P, S // P], F32, name="gate2")
-        ident = keep.tile([P, P], F32, name="ident", align_bytes=64)
+        dy_w = place("dy_w", [P, T], I32, None)
+        dy_s = place("dy_s", [P, T], U8, None)
+        gate_rows = place("gate_rows", [P, P], F32, None)
+        gate2 = place("gate2", [P, S // P], F32, None)
+        ident = place("ident", [P, P], F32, None)
 
-        nc.gpsimd.memset(dy_s[:].bitcast(I32), 0)
+        w2_raw, a_sb, w1_raw = {}, {}, {}
+        turned, w2_mx, g_words, g_scales, da, da_mx, w1_mx = {}, {}, {}, {}, {}, {}, {}
+
+        def load_w2(e):
+            w2_raw[e] = place("w2_raw%d" % e, [P, PACK, H], F32, W2_AT + e * MATRIX)
+            nc.sync.dma_start(w2_raw[e][:], w2[e].rearrange("(p j) i -> p j i", j=PACK))
+
+        def load_a(e):
+            a_sb[e] = place("a%d" % e, [P, PACK, C], F32, A_AT + e * MATRIX)
+            nc.sync.dma_start(a_sb[e][:], a[:, e * C : (e + 1) * C].rearrange("(p j) s -> p j s", j=PACK))
+
+        def load_w1(e, first, last, offset=None):
+            offset = W1_AT + e * MATRIX + first * QUARTER if offset is None else offset
+            raw = place("w1_raw%d%d" % (e, first), [P, PACK, (last - first) * P], F32, offset)
+            nc.sync.dma_start(raw[:], w1[e][:, first * P : last * P].rearrange("(p j) k -> p j k", j=PACK))
+            for kb in range(first, last):
+                w1_raw[e, kb] = raw[:, :, (kb - first) * P : (kb - first + 1) * P]
+
         nc.gpsimd.memset(gate_rows[:], 0.0)
         make_identity(nc, ident[:])
         nc.sync.dma_start(offs_sb[:], offs)
-        for r in range(4):
-            nc.sync.dma_start(dy_s[r:P:32, :].bitcast(I32), dy_scales[0, r:16:4, :].bitcast(I32))
+        for q in range(4):
+            rows = dy_scales[0, 4 * q : 4 * q + 4, :].bitcast(I32)
+            nc.sync.dma_start(dy_s[32 * q : 32 * (q + 1), :].bitcast(I32), rows.unsqueeze(0).broadcast_to([8, 4, T // 4]))
+        load_w2(0)
+        nc.sync.dma_start(dy_w[:], dy_words[0].rearrange("p t d -> p (t d)").bitcast(I32))
+        nc.sync.dma_start(gate_rows[0 : S // P, :], gate[0].rearrange("(c s) -> c s", s=P))
+        load_w2(1)
+        load_w2(2)
+        load_a(0)
+        load_w2(3)
+        load_a(1)
+        load_w2(4)
+        load_a(2)
+        load_a(3)
+        load_w1(0, 0, 1)
+        load_w1(1, 0, 1)
+        load_a(4)
+        for e in range(2, E):
+            load_w1(e, 0, 1)
         nc.sync.dma_start(pos1_sb[:], pos1)
         nc.sync.dma_start(pos2_sb[:], pos2)
+        for e in range(2, E):
+            load_w1(e, 1, 2)
+        for e in range(2):
+            load_w1(e, 1, 2, PAIR_AT + e * QUARTER)
+        for e in range(E):
+            load_w1(e, 2, 4)
 
-        w2_raw, a_sb, w1_raw = {}, {}, {}
-        turned, w1_far = {}, {}
-        w2_mx, g_words, g_scales, da, da_mx, w1_mx = {}, {}, {}, {}, {}, {}
-
-        w1_pair = place("w1_pair", [P, 2, PACK, P], F32, PAIR)
-        for item in LOADS.split():
-            if item == "d":
-                nc.sync.dma_start(dy_w[:], dy_words[0].rearrange("p t d -> p (t d)").bitcast(I32))
-            elif item == "g":
-                nc.sync.dma_start(gate_rows[0 : S // P, :], gate[0].rearrange("(c s) -> c s", s=P))
-                gate_t = psum.tile([P, PACK, P], F32, name="turned", tag="turned", bufs=4)
-                nc.tensor.transpose(gate_t[:, 0, :], gate_rows[:], ident[:])
-                nc.scalar.activation(gate2[:], gate_t[:, 0, 0 : S // P], COPY, scale=2.0)
-            elif item[0] == "w":
-                e = int(item[1])
-                w2_raw[e] = place("w2_raw%d" % e, [P, PACK, H], F32, W_ROWS + e * 8192)
-                nc.sync.dma_start(w2_raw[e][:], w2[e].rearrange("(p j) i -> p j i", j=PACK))
-            elif item[0] in ("a", "b", "c"):
-                e = int(item[1])
-                lo, hi = {"a": (0, C), "b": (0, C // 2), "c": (C // 2, C)}[item[0]]
-                rows = place("a_" + item, [P, PACK, hi - lo], F32, A_ROWS + e * 8192 + lo * 16)
-                nc.sync.dma_start(rows[:], a[:, e * C + lo : e * C + hi].rearrange("(p j) s -> p j s", j=PACK))
-                for c in range(lo // P, hi // P):
-                    a_sb[e, c] = rows[:, :, c * P - lo : (c + 1) * P - lo]
-            else:
-                e = int(item[1])
-                lo, hi = {"q": (0, P), "r": (P, 2 * P), "n": (0, 2 * P), "f": (2 * P, K), "t": (P, K)}[item[0]]
-                if item in ("r0", "r1"):
-                    raw = w1_pair[:, e]
-                else:
-                    raw = place("w1_raw_" + item, [P, PACK, hi - lo], F32, W1_ROWS + e * 8192 + lo * 16)[:]
-                w1_far[e] = raw
-                nc.sync.dma_start(raw, w1[e][:, lo:hi].rearrange("(p j) k -> p j k", j=PACK))
-                for kb in range(lo // P, hi // P):
-                    w1_raw[e, kb] = raw[:, :, kb * P - lo : (kb + 1) * P - lo]
+        gate_t = psum.tile([P, PACK, P], F32, name="turned", tag="turned", bufs=4)
+        nc.tensor.transpose(gate_t[:, 0, :], gate_rows[:], ident[:])
 
         def interleave(copy, dst, src):
             copy(dst.rearrange("p (c i) j -> p c j i", i=2), src.rearrange("p j (c i) -> p c j i", i=2))
 
-        def quantize(codes, scales, rounded, fmt):
-            nc.vector.quantize_mx(out=codes.bitcast(fmt), scales=scales, in_=rounded.rearrange("p c j -> p (c j)"))
-
-        def gather(got, window, e):
-            nc.vector.tensor_copy(got[:], window.indirect(offs_sb[:, e * C // 16 : (e + 1) * C // 16]))
-            return got
+        def quantize(name, rounded, fmt, codes_at, scales_at=None):
+            width = rounded.shape[1]
+            codes = place(name + "_codes", [P, width], U32, codes_at)
+            scales = place(name + "_scales", [P, width], U8, scales_at)
+            nc.vector.quantize_mx(out=codes[:].bitcast(fmt), scales=scales[:], in_=rounded.rearrange("p c j -> p (c j)"))
+            return codes, scales
 
         def gather_words(e, offset):
-            g_words[e] = gather(place("g_words%d" % e, [P, C], U32, offset), dy_w[:].bitcast(U32), e)
+            g_words[e] = place("g_words%d" % e, [P, C], U32, offset)
+            nc.vector.tensor_copy(g_words[e][:], dy_w[:].bitcast(U32).indirect(offs_sb[:, e * C // 16 : (e + 1) * C // 16]))
 
-        def prepare_w2(e, rounded_at, codes_at):
-            rounded = place("w2_bf%d" % e, [P, H, PACK], BF16, rounded_at)
+        def gather_scales(e, offset):
+            g_scales[e] = place("g_scales%d" % e, [P, C], U8, offset)
+            nc.vector.tensor_copy(g_scales[e][:], dy_s[:].indirect(offs_sb[:, e * C // 16 : (e + 1) * C // 16]))
+
+        def round_w2(e, on_gpsimd=False):
+            rounded = place("w2_bf%d" % e, [P, H, PACK], BF16, turn(max(e - 1, 0)))
             for h in range(2):
                 cols = slice(h * H // 2, (h + 1) * H // 2)
-                interleave(nc.scalar.copy, rounded[:, cols, :], w2_raw[e][:, :, cols])
-            codes = place("w2_codes%d" % e, [P, H], U32, codes_at)
-            scales = place("w2_scales%d" % e, [P, H], U8, period(e + 1) + 2048 if e + 1 < E else W_ROWS + E * 8192 + 512)
-            quantize(codes[:], scales[:], rounded[:], E4M3)
-            w2_mx[e] = codes, scales
+                if on_gpsimd:
+                    nc.gpsimd.tensor_scalar(
+                        rounded[:, cols, :], w2_raw[e][:, :, cols].rearrange("p j c -> p c j"), 1.0, 0.0, ALU.mult, ALU.add
+                    )
+                else:
+                    interleave(nc.scalar.copy, rounded[:, cols, :], w2_raw[e][:, :, cols])
+            return rounded
+
+        def quantize_w2(e, rounded):
+            w2_mx[e] = quantize("w2_%d" % e, rounded[:], E4M3, slopes_at(e - 2) + 2 * QUARTER if e >= 2 else None)
 
         def round_w1(experts, kb, copy, rounded_at):
-            rounded = place("w1_%d_%d_bf" % (kb, experts[0]), [P, len(experts) * P, PACK], BF16, rounded_at)
+            rounded = place("w1_bf%d%d" % (kb, experts[0]), [P, len(experts) * P, PACK], BF16, rounded_at)
             for n, e in enumerate(experts):
                 interleave(copy, rounded[:, n * P : (n + 1) * P, :], w1_raw[e, kb])
             return rounded
 
-        def prepare_w1(experts, kb, copy, rounded_at, codes_at):
-            quantize_w1(experts, kb, round_w1(experts, kb, copy, rounded_at), codes_at)
-
-        def quantize_w1(experts, kb, rounded, codes_at, scales_at=None):
-            width = len(experts) * P
-            name = "w1_%d_%d" % (kb, experts[0])
-            codes = place(name + "_codes", [P, width], U32, codes_at)
-            if scales_at is None:
-                scales = keep.tile([P, width], U8, name=name + "_scales", align_bytes=64)
-            else:
-                scales = place(name + "_scales", [P, width], U8, scales_at)
-            quantize(codes[:], scales[:], rounded[:], E4M3)
+        def quantize_w1(experts, kb, rounded, codes_at=None):
+            codes, scales = quantize("w1_%d%d" % (kb, experts[0]), rounded[:], E4M3, codes_at)
             for n, e in enumerate(experts):
                 w1_mx[e, kb] = codes[:, n * P : (n + 1) * P], scales[:, n * P : (n + 1) * P]
 
-        def prepare_far(experts, rounded_at, codes_at):
-            width = len(experts) * 2 * P
-            name = "w1_far%d" % experts[0]
-            rounded = place(name + "_bf", [P, width, PACK], BF16, rounded_at)
-            for n, e in enumerate(experts):
-                interleave(nc.scalar.copy, rounded[:, n * 2 * P : (n + 1) * 2 * P, :], w1_far[e])
-            codes = place(name + "_codes", [P, width], U32, codes_at)
-            scales = keep.tile([P, width], U8, name=name + "_scales", align_bytes=64)
-            quantize(codes[:], scales[:], rounded[:], E4M3)
-            for n in range(width // P):
-                w1_mx[experts[n // 2], 2 + n % 2] = codes[:, n * P : (n + 1) * P], scales[:, n * P : (n + 1) * P]
-
         def quantize_da(e):
-            codes = place("da_codes%d" % e, [P, C], U32, A_ROWS + e * 8192)
-            scales = place("da_scales%d" % e, [P, C], U8, A_ROWS + e * 8192 + 2048)
-            quantize(codes[:], scales[:], da[e][:], E5M2)
-            da_mx[e] = codes, scales
+            da_mx[e] = quantize("da%d" % e, da[e][:, 0], E5M2, A_AT + e * MATRIX, A_AT + e * MATRIX + QUARTER)
 
-        def front(e):
-            sums = four_banks(e)
+        def first_layer(e):
+            sums = [psum.tile([P, H], F32, name="sums", tag="sums", bufs=4) for c in range(CHUNKS)]
             for c in range(CHUNKS):
                 cols = slice(c * P, (c + 1) * P)
                 nc.tensor.matmul_mx(
-                    out=sums[c],
+                    out=sums[c][:],
                     lhsT=g_words[e][:, cols].bitcast(E5M2),
                     lhsT_scale=g_scales[e][:, cols],
                     rhs=w2_mx[e][0][:].bitcast(E4M3),
@@ -189,127 +180,121 @@ def tile_moe_bdx_mlp_relu2_kernel(
                     stop=True,
                 )
             for c in range(CHUNKS):
-                if e + 1 == E and c < 2:
-                    dh = place("dh_last%d" % c, [P, PACK, P], F32, W1_ROWS + c * 8192)
-                else:
-                    dh = keep.tile([P, PACK, P], F32, name="dh", bufs=6, align_bytes=64)
+                dh = keep.tile([P, PACK, P], F32, name="dh", bufs=6, align_bytes=64)
                 col = e * CHUNKS + c
                 nc.scalar.activation(
-                    dh[:], sums[c].rearrange("s (p j) -> s j p", j=PACK), COPY, scale=gate2[:, col : col + 1]
+                    dh[:], sums[c][:].rearrange("s (p j) -> s j p", j=PACK), COPY, scale=gate2[:, col : col + 1]
                 )
                 turned[e, c] = psum.tile([P, PACK, P], F32, name="turned", tag="turned", bufs=4)
                 for j in range(PACK):
                     nc.tensor.transpose(turned[e, c][:, j, :], dh[:, j, :], ident[:])
 
-        def product(e, c):
-            if c == 0:
-                da[e] = place("da%d" % e, [P, C, PACK], BF16, period(e) + DA)
-            cols = slice(c * P, (c + 1) * P)
-            if c >= HOPS[e]:
-                slope = place("slope%d%d" % (e, c), [P, PACK, P], F32, period(e - 1) + SLOPE + (c - 1) * 2048)
-                nc.gpsimd.tensor_scalar(slope[:], a_sb[e, c], FLOAT_MAX, 0.0, ALU.min, ALU.max)
-                nc.vector.tensor_tensor(
-                    da[e][:, cols, :].rearrange("p (c i) j -> p c j i", i=2),
-                    slope[:].rearrange("p j (c i) -> p c j i", i=2),
-                    turned[e, c][:].rearrange("p j (c i) -> p c j i", i=2),
-                    ALU.mult,
+        def products(e):
+            da[e] = place("da%d" % e, [P, 2, C, PACK], BF16, turn(e))
+            for c in range(CHUNKS):
+                cols = slice(c * P, (c + 1) * P)
+                if c >= FUSED[e]:
+                    slope = place("slope%d%d" % (e, c), [P, PACK, P], F32, slopes_at(e) + c * QUARTER)
+                    nc.gpsimd.tensor_scalar(slope[:], a_sb[e][:, :, cols], FLOAT_MAX, 0.0, ALU.min, ALU.max)
+                    nc.vector.tensor_tensor(
+                        da[e][:, 0, cols, :].rearrange("p (c i) j -> p c j i", i=2),
+                        slope[:].rearrange("p j (c i) -> p c j i", i=2),
+                        turned[e, c][:].rearrange("p j (c i) -> p c j i", i=2),
+                        ALU.mult,
+                    )
+                else:
+                    nc.vector.scalar_tensor_tensor(
+                        out=da[e][:, 0, cols, :],
+                        in0=a_sb[e][:, :, cols].rearrange("p j s -> p s j"),
+                        scalar=0.0,
+                        in1=turned[e, c][:].rearrange("p j s -> p s j"),
+                        op0=ALU.max,
+                        op1=ALU.mult,
+                    )
+
+        def second_layer(kb):
+            accs = []
+            for e in range(E):
+                ring = "sums" if e + 1 < E else "turned"
+                acc = psum.tile([P, C], F32, name=ring, tag=ring, bufs=4)
+                codes, scales = w1_mx[e, kb]
+                nc.tensor.matmul_mx(
+                    out=acc[:],
+                    lhsT=codes.bitcast(E4M3),
+                    lhsT_scale=scales,
+                    rhs=da_mx[e][0][:].bitcast(E5M2),
+                    rhs_scale=da_mx[e][1][:],
+                    start=True,
+                    stop=True,
                 )
-            else:
-                nc.vector.scalar_tensor_tensor(
-                    out=da[e][:, cols, :],
-                    in0=a_sb[e, c].rearrange("p j s -> p s j"),
-                    scalar=0.0,
-                    in1=turned[e, c][:].rearrange("p j s -> p s j"),
-                    op0=ALU.max,
-                    op1=ALU.mult,
-                )
+                accs.append(acc)
+            for e in range(E):
+                nc.scalar.copy(dx[kb][:, e * C : (e + 1) * C], accs[e][:])
 
-        def second_layer(e, kb):
-            acc = psum.tile([P, C], F32, name="acc", tag="turned", bufs=4)[:]
-            second_matmul(e, kb, acc)
-            nc.scalar.copy(dx[kb][:, e * C : (e + 1) * C], acc)
+        spare = [A_AT + e * MATRIX + (1 + h) * 2560 for e in range(E) for h in range(2)]
 
-        def second_matmul(e, kb, acc):
-            codes, scales = w1_mx[e, kb]
-            nc.tensor.matmul_mx(
-                out=acc,
-                lhsT=codes.bitcast(E4M3),
-                lhsT_scale=scales,
-                rhs=da_mx[e][0][:].bitcast(E5M2),
-                rhs_scale=da_mx[e][1][:],
-                start=True,
-                stop=True,
-            )
+        def gather_first(kb, h, offset):
+            first = place("first%d%d" % (kb, h), [P, HALF], F32, offset)
+            nc.vector.tensor_copy(first[:], dx[kb][:].indirect(pos1_sb[:, h * HALF // 16 : (h + 1) * HALF // 16]))
+            return first
 
-        def staging(n):
-            return A_ROWS + n % 10 // 2 * 8192 + 2560 + n % 2 * 2560
+        def gather_second(kb, lo, hi, firsts, offset):
+            first = firsts[lo // HALF][:, lo % HALF : lo % HALF + hi - lo]
+            total = place("total%d%d" % (kb, lo), [P, hi - lo], F32, offset)
+            nc.vector.tensor_tensor(total[:], dx[kb][:].indirect(pos2_sb[:, lo // 16 : hi // 16]), first, ALU.add)
+            nc.sync.dma_start(out[kb * P : (kb + 1) * P, lo:hi], total[:])
 
-        held = {(0, 1): PAIR - 512, (0, 2): PAIR + 2048, (1, 1): W1_ROWS + 8192 + 4096, (1, 2): W1_ROWS + 3 * 8192 + 4096, (1, 3): W1_ROWS + 4 * 8192 + 4096}
-
-        def combine(kb):
-            cuts = [0, T // 2, T] if kb + 1 < BLOCKS else [0, T // 2, T - 256, T - 128, T]
-            firsts = []
-            for h in range(2):
-                first = place("first%d%d" % (kb, h), [P, T // 2], F32, held.get((kb, h), staging(4 * kb + h)))
-                nc.vector.tensor_copy(first[:], dx[kb][:].indirect(pos1_sb[:, h * T // 32 : (h + 1) * T // 32]))
-                firsts.append(first)
-            for n, (lo, hi) in enumerate(zip(cuts, cuts[1:])):
-                first = firsts[lo // (T // 2)][:, lo % (T // 2) : lo % (T // 2) + hi - lo]
-                total = place("total%d%d" % (kb, n), [P, hi - lo], F32, held.get((kb, 2 + n), staging(4 * kb + 2 + n)))
-                nc.vector.tensor_tensor(total[:], dx[kb][:].indirect(pos2_sb[:, lo // 16 : hi // 16]), first, ALU.add)
-                nc.sync.dma_start(out[kb * P : (kb + 1) * P, lo:hi], total[:])
-
-        for e in range(E - 1):
-            g_scales[e] = gather(keep.tile([P, C], U8, name="g_scales%d" % e, align_bytes=64), dy_s[:], e)
-        gather_words(0, 4096)
-        prepare_w2(0, 0, 6144)
-        gather_words(1, 0)
-        prepare_w2(1, period(-1) + DA, 8192)
-        g_scales[E - 1] = gather(place("g_scales_last", [P, C], U8, W_ROWS + E * 8192), dy_s[:], E - 1)
-        gather_words(2, W_ROWS + 8192)
-        front(0)
-        for c in range(CHUNKS):
-            product(0, c)
+        for e in range(3):
+            gather_scales(e, None)
+        gather_words(0, None)
+        quantize_w2(0, round_w2(0))
+        nc.scalar.activation(gate2[:], gate_t[:, 0, 0 : S // P], COPY, scale=2.0)
+        gather_words(1, W2_AT)
+        gather_scales(3, W2_AT + QUARTER)
+        gather_words(2, W2_AT + 2 * QUARTER)
+        first_layer(0)
+        quantize_w2(1, round_w2(1, on_gpsimd=True))
+        gather_scales(4, W2_AT + MATRIX)
+        gather_words(3, W2_AT + MATRIX + QUARTER)
+        products(0)
         for e in range(1, E):
             if e + 1 < E:
-                prepare_w2(e + 1, period(e) + ROUNDED, A_ROWS + e * 8192 - 2048)
+                quantize_w2(e + 1, round_w2(e + 1))
             else:
-                prepare_w1([0, 1], 0, nc.scalar.copy, period(e) + 2048, A_ROWS + e * 8192 - 2048)
-            front(e)
+                quantize_w1([0, 1], 0, round_w1([0, 1], 0, nc.scalar.copy, turn(e)), slopes_at(e - 1) + 2 * QUARTER)
+            first_layer(e)
             quantize_da(e - 1)
-            if e + 2 < E:
-                gather_words(e + 2, period(e) + WORDS)
-            for c in range(CHUNKS):
-                product(e, c)
-        dx = [place("dx%d" % kb, [P, S], F32, W_ROWS + kb * 10240) for kb in range(BLOCKS)]
-        last = A_ROWS + E * 8192
-        spent = A_ROWS + 3 * 8192 - 2048
-        prepare_w1([2, 3], 0, nc.scalar.copy, spent, last - 1024)
+            if e == 1:
+                gather_words(E - 1, FIRST_AT + 3 * QUARTER)
+            products(e)
+
+        dx = [place("dx%d" % kb, [P, S], F32, W2_AT + kb * S * 4) for kb in range(BLOCKS)]
+        last = slopes_at(E - 1) + 2 * QUARTER
+        quantize_w1([2, 3], 0, round_w1([2, 3], 0, nc.scalar.copy, FIRST_AT), last)
+        rounded = round_w1([4], 0, nc.scalar.copy, FIRST_AT + QUARTER)
         quantize_da(E - 1)
-        rounded4 = round_w1([4], 0, nc.vector.tensor_copy, spent + 512)
-        single = round_w1([2], 1, nc.vector.tensor_copy, spent - 960)
-        quantize_w1([4], 0, rounded4, last - 1536)
-        waiting = four_banks(E)
-        waiting = waiting[2:] + waiting[:2]
-        for e in range(E - 1):
-            second_matmul(e, 0, waiting[e])
-        acc = psum.tile([P, C], F32, name="acc", tag="turned", bufs=4)[:]
-        second_matmul(E - 1, 0, acc)
-        for e in range(E - 1):
-            nc.scalar.copy(dx[0][:, e * C : (e + 1) * C], waiting[e])
-        nc.scalar.copy(dx[0][:, (E - 1) * C :], acc)
-        pair = round_w1([3, 4], 1, nc.vector.tensor_copy, spent - 2944)
-        quantize_w1([2], 1, single, 8192)
-        quantize_w1([3, 4], 1, pair, 6144)
-        prepare_w1([0, 1], 1, nc.scalar.copy, last - 3008, period(3))
-        for e in range(E):
-            second_layer(e, 1)
-        combine(0)
-        prepare_far([0, 1], 7104, period(1))
-        prepare_far([2, 3], W1_ROWS + 4096, period(1) + 2048)
-        prepare_far([4], W1_ROWS + 2 * 8192 + 4096, period(1) + 4096)
-        combine(1)
-        for kb in range(2, BLOCKS):
-            for e in range(E):
-                second_layer(e, kb)
-            combine(kb)
+        quantize_w1([4], 0, rounded, last + QUARTER // 2)
+        second_layer(0)
+        pair = round_w1([2, 3], 1, nc.vector.tensor_copy, turn(E - 1) + 2 * QUARTER)
+        single = round_w1([4], 1, nc.vector.tensor_copy, turn(E - 1) + 3 * QUARTER)
+        quantize_w1([2, 3], 1, pair)
+        quantize_w1([4], 1, single)
+        for kb in range(BLOCKS):
+            firsts = [gather_first(kb, 0, spare[2 * kb])]
+            if kb == 0:
+                held = PAIR_AT + 512
+                quantize_w1([0, 1], 1, round_w1([0, 1], 1, nc.scalar.copy, FIRST_AT + 2 * QUARTER))
+            elif kb + 1 < BLOCKS:
+                held = turn(kb + 1)
+                quantize_w1([0, 1, 2, 3], kb + 1, round_w1([0, 1, 2, 3], kb + 1, nc.scalar.copy, held + 512))
+                quantize_w1([4], kb + 1, round_w1([4], kb + 1, nc.scalar.copy, held + 5632))
+            if kb + 1 < BLOCKS:
+                second_layer(kb + 1)
+                firsts.append(gather_first(kb, 1, held))
+                gather_second(kb, 0, HALF, firsts, held + 2560)
+                gather_second(kb, HALF, T, firsts, spare[2 * kb + 1])
+            else:
+                firsts.append(gather_first(kb, 1, spare[7]))
+                cuts = [0, HALF, T - 2 * P, T - P, T]
+                for n, (lo, hi) in enumerate(zip(cuts, cuts[1:])):
+                    gather_second(kb, lo, hi, firsts, spare[(8 + n) % 10])

@@ -34,7 +34,7 @@ A_AT = W2_AT + E * MATRIX
 W1_AT = A_AT + E * MATRIX
 FIRST_AT = W1_AT + E * MATRIX
 TURN_AT = FIRST_AT + MATRIX
-PAIR_AT = TURN_AT + 3 * MATRIX
+PIECE = 256
 
 
 def tile_moe_bdx_mlp_relu2_kernel(
@@ -78,12 +78,11 @@ def tile_moe_bdx_mlp_relu2_kernel(
             a_sb[e] = place("a%d" % e, [P, PACK, C], F32, A_AT + e * MATRIX)
             nc.sync.dma_start(a_sb[e][:], a[:, e * C : (e + 1) * C].rearrange("(p j) s -> p j s", j=PACK))
 
-        def load_w1(e, first, last, offset=None):
-            offset = W1_AT + e * MATRIX + first * QUARTER if offset is None else offset
+        def load_w1(e, first, last):
+            offset = W1_AT + e * MATRIX + first * QUARTER
             raw = place("w1_raw%d%d" % (e, first), [P, PACK, (last - first) * P], F32, offset)
             nc.sync.dma_start(raw[:], w1[e][:, first * P : last * P].rearrange("(p j) k -> p j k", j=PACK))
-            for kb in range(first, last):
-                w1_raw[e, kb] = raw[:, :, (kb - first) * P : (kb - first + 1) * P]
+            w1_raw[e, first] = raw
 
         nc.gpsimd.memset(gate_rows[:], 0.0)
         make_identity(nc, ident[:])
@@ -109,10 +108,8 @@ def tile_moe_bdx_mlp_relu2_kernel(
             load_w1(e, 0, 1)
         nc.sync.dma_start(pos1_sb[:], pos1)
         nc.sync.dma_start(pos2_sb[:], pos2)
-        for e in range(2, E):
+        for e in range(E):
             load_w1(e, 1, 2)
-        for e in range(2):
-            load_w1(e, 1, 2, PAIR_AT + e * QUARTER)
         for e in range(E):
             load_w1(e, 2, 4)
 
@@ -153,15 +150,18 @@ def tile_moe_bdx_mlp_relu2_kernel(
             w2_mx[e] = quantize("w2_%d" % e, rounded[:], E4M3, slopes_at(e - 2) + 2 * QUARTER if e >= 2 else None)
 
         def round_w1(experts, kb, copy, rounded_at):
-            rounded = place("w1_bf%d%d" % (kb, experts[0]), [P, len(experts) * P, PACK], BF16, rounded_at)
+            width = w1_raw[experts[0], kb].shape[2]
+            rounded = place("w1_bf%d%d" % (kb, experts[0]), [P, len(experts) * width, PACK], BF16, rounded_at)
             for n, e in enumerate(experts):
-                interleave(copy, rounded[:, n * P : (n + 1) * P, :], w1_raw[e, kb])
+                interleave(copy, rounded[:, n * width : (n + 1) * width, :], w1_raw[e, kb][:])
             return rounded
 
         def quantize_w1(experts, kb, rounded, codes_at=None):
             codes, scales = quantize("w1_%d%d" % (kb, experts[0]), rounded[:], E4M3, codes_at)
-            for n, e in enumerate(experts):
-                w1_mx[e, kb] = codes[:, n * P : (n + 1) * P], scales[:, n * P : (n + 1) * P]
+            blocks = rounded.shape[1] // P // len(experts)
+            for n in range(rounded.shape[1] // P):
+                cols = slice(n * P, (n + 1) * P)
+                w1_mx[experts[n // blocks], kb + n % blocks] = codes[:, cols], scales[:, cols]
 
         def quantize_da(e):
             da_mx[e] = quantize("da%d" % e, da[e][:, 0], E5M2, A_AT + e * MATRIX, A_AT + e * MATRIX + QUARTER)
@@ -212,11 +212,10 @@ def tile_moe_bdx_mlp_relu2_kernel(
                         op1=ALU.mult,
                     )
 
-        def second_layer(kb):
+        def second_layer(kb, rings, on_vector=0):
             accs = []
             for e in range(E):
-                ring = "sums" if e + 1 < E else "turned"
-                acc = psum.tile([P, C], F32, name=ring, tag=ring, bufs=4)
+                acc = psum.tile([P, C], F32, name=rings[e], tag=rings[e], bufs=4)
                 codes, scales = w1_mx[e, kb]
                 nc.tensor.matmul_mx(
                     out=acc[:],
@@ -229,20 +228,27 @@ def tile_moe_bdx_mlp_relu2_kernel(
                 )
                 accs.append(acc)
             for e in range(E):
-                nc.scalar.copy(dx[kb][:, e * C : (e + 1) * C], accs[e][:])
+                copy = nc.vector.tensor_copy if e < on_vector else nc.scalar.copy
+                copy(dx[kb][:, e * C : (e + 1) * C], accs[e][:])
 
         spare = [A_AT + e * MATRIX + (1 + h) * 2560 for e in range(E) for h in range(2)]
 
-        def gather_first(kb, h, offset):
-            first = place("first%d%d" % (kb, h), [P, HALF], F32, offset)
-            nc.vector.tensor_copy(first[:], dx[kb][:].indirect(pos1_sb[:, h * HALF // 16 : (h + 1) * HALF // 16]))
+        def gather_first(kb, lo, hi, offset):
+            first = place("first%d_%d" % (kb, lo), [P, hi - lo], F32, offset)
+            nc.scalar.activation(first[:], dx[kb][:].indirect(pos1_sb[:, lo // 16 : hi // 16]), COPY)
             return first
 
-        def gather_second(kb, lo, hi, firsts, offset):
-            first = firsts[lo // HALF][:, lo % HALF : lo % HALF + hi - lo]
-            total = place("total%d%d" % (kb, lo), [P, hi - lo], F32, offset)
-            nc.vector.tensor_tensor(total[:], dx[kb][:].indirect(pos2_sb[:, lo // 16 : hi // 16]), first, ALU.add)
+        def gather_second(kb, lo, first, offset):
+            hi = lo + first.shape[1]
+            total = place("total%d_%d" % (kb, lo), [P, hi - lo], F32, offset)
+            nc.vector.tensor_tensor(total[:], dx[kb][:].indirect(pos2_sb[:, lo // 16 : hi // 16]), first[:], ALU.add)
             nc.sync.dma_start(out[kb * P : (kb + 1) * P, lo:hi], total[:])
+
+        def combine(kb, width, firsts_at, totals_at):
+            cuts = range(0, T, width)
+            firsts = [gather_first(kb, lo, lo + width, firsts_at + lo * 4) for lo in cuts]
+            for lo, first in zip(cuts, firsts):
+                gather_second(kb, lo, first, totals_at + lo * 4)
 
         for e in range(3):
             gather_scales(e, None)
@@ -274,27 +280,22 @@ def tile_moe_bdx_mlp_relu2_kernel(
         rounded = round_w1([4], 0, nc.scalar.copy, FIRST_AT + QUARTER)
         quantize_da(E - 1)
         quantize_w1([4], 0, rounded, last + QUARTER // 2)
-        second_layer(0)
-        pair = round_w1([2, 3], 1, nc.vector.tensor_copy, turn(E - 1) + 2 * QUARTER)
-        single = round_w1([4], 1, nc.vector.tensor_copy, turn(E - 1) + 3 * QUARTER)
-        quantize_w1([2, 3], 1, pair)
+        usual = ["sums"] * (E - 1) + ["turned"]
+        second_layer(0, usual)
+        four = round_w1([0, 1, 2, 3], 1, nc.vector.tensor_copy, turn(E - 1) + 2 * QUARTER)
+        single = round_w1([4], 1, nc.vector.tensor_copy, turn(E - 1))
+        quantize_w1([0, 1, 2, 3], 1, four)
         quantize_w1([4], 1, single)
-        for kb in range(BLOCKS):
-            firsts = [gather_first(kb, 0, spare[2 * kb])]
-            if kb == 0:
-                held = PAIR_AT + 512
-                quantize_w1([0, 1], 1, round_w1([0, 1], 1, nc.scalar.copy, FIRST_AT + 2 * QUARTER))
-            elif kb + 1 < BLOCKS:
-                held = turn(kb + 1)
-                quantize_w1([0, 1, 2, 3], kb + 1, round_w1([0, 1, 2, 3], kb + 1, nc.scalar.copy, held + 512))
-                quantize_w1([4], kb + 1, round_w1([4], kb + 1, nc.scalar.copy, held + 5632))
-            if kb + 1 < BLOCKS:
-                second_layer(kb + 1)
-                firsts.append(gather_first(kb, 1, held))
-                gather_second(kb, 0, HALF, firsts, held + 2560)
-                gather_second(kb, HALF, T, firsts, spare[2 * kb + 1])
-            else:
-                firsts.append(gather_first(kb, 1, spare[7]))
-                cuts = [0, HALF, T - 2 * P, T - P, T]
-                for n, (lo, hi) in enumerate(zip(cuts, cuts[1:])):
-                    gather_second(kb, lo, hi, firsts, spare[(8 + n) % 10])
+        combine(0, HALF, spare[0], spare[2])
+        second_layer(1, usual)
+        far = [round_w1(pair, 2, nc.vector.tensor_copy, turn(2) + n * 2 * QUARTER) for n, pair in enumerate(([0, 1], [2, 3]))]
+        last_far = W1_AT + 4 * MATRIX + 2 * QUARTER
+        far.append(round_w1([4], 2, nc.vector.tensor_copy, turn(3)))
+        quantize_w1([0, 1], 2, far[0], W1_AT + 2 * MATRIX + 2 * QUARTER)
+        quantize_w1([2, 3], 2, far[1], last_far + 2624)
+        quantize_w1([4], 2, far[2])
+        combine(1, HALF, spare[4], last_far - 2496)
+        second_layer(2, usual)
+        combine(2, HALF, spare[6], spare[8])
+        second_layer(3, ["turned"] * 3 + ["sums"] * 2, on_vector=2)
+        combine(3, PIECE, spare[0], spare[4])

@@ -34,6 +34,7 @@ A_AT = W2_AT + E * MATRIX
 W1_AT = A_AT + E * MATRIX
 FIRST_AT = W1_AT + E * MATRIX
 TURN_AT = FIRST_AT + MATRIX
+SUMS_AT = TURN_AT + 3 * MATRIX
 PIECE = 256
 
 
@@ -78,8 +79,8 @@ def tile_moe_bdx_mlp_relu2_kernel(
             a_sb[e] = place("a%d" % e, [P, PACK, C], F32, A_AT + e * MATRIX)
             nc.sync.dma_start(a_sb[e][:], a[:, e * C : (e + 1) * C].rearrange("(p j) s -> p j s", j=PACK))
 
-        def load_w1(e, first, last):
-            offset = W1_AT + e * MATRIX + first * QUARTER
+        def load_w1(e, first, last, offset=None):
+            offset = W1_AT + e * MATRIX + first * QUARTER if offset is None else offset
             raw = place("w1_raw%d%d" % (e, first), [P, PACK, (last - first) * P], F32, offset)
             nc.sync.dma_start(raw[:], w1[e][:, first * P : last * P].rearrange("(p j) k -> p j k", j=PACK))
             w1_raw[e, first] = raw
@@ -109,7 +110,7 @@ def tile_moe_bdx_mlp_relu2_kernel(
         nc.sync.dma_start(pos1_sb[:], pos1)
         nc.sync.dma_start(pos2_sb[:], pos2)
         for e in range(E):
-            load_w1(e, 1, 2)
+            load_w1(e, 1, 2, SUMS_AT + 1536 if e + 1 == E else None)
         for e in range(E):
             load_w1(e, 2, 4)
 
@@ -286,7 +287,7 @@ def tile_moe_bdx_mlp_relu2_kernel(
         single = round_w1([4], 1, nc.vector.tensor_copy, turn(E - 1))
         quantize_w1([0, 1, 2, 3], 1, four)
         quantize_w1([4], 1, single)
-        combine(0, HALF, spare[0], spare[2])
+        combine(0, HALF, spare[0], SUMS_AT)
         second_layer(1, usual)
         far = [round_w1(pair, 2, nc.vector.tensor_copy, turn(2) + n * 2 * QUARTER) for n, pair in enumerate(([0, 1], [2, 3]))]
         last_far = W1_AT + 4 * MATRIX + 2 * QUARTER

@@ -25,7 +25,7 @@ CHUNKS = C // P
 BLOCKS = K // P
 HALF = T // 2
 FLOAT_MAX = 3.4028234663852886e38
-FUSED = (0, 0, 2, 2, 2)
+FUSED = (0, 2, 2, 2, 2)
 
 MATRIX = 8192
 QUARTER = MATRIX // 4
@@ -68,7 +68,7 @@ def tile_moe_bdx_mlp_relu2_kernel(
         gate2 = place("gate2", [P, S // P], F32, None)
         ident = place("ident", [P, P], F32, None)
 
-        w2_raw, a_sb, w1_raw = {}, {}, {}
+        w2_raw, a_sb, w1_raw, moved = {}, {}, {}, {}
         turned, w2_mx, g_words, g_scales, da, da_mx, w1_mx = {}, {}, {}, {}, {}, {}, {}
 
         def load_w2(e):
@@ -189,6 +189,9 @@ def tile_moe_bdx_mlp_relu2_kernel(
                 turned[e, c] = psum.tile([P, PACK, P], F32, name="turned", tag="turned", bufs=4)
                 for j in range(PACK):
                     nc.tensor.transpose(turned[e, c][:, j, :], dh[:, j, :], ident[:])
+                if (e, c) == (0, CHUNKS - 1):
+                    moved[e, c] = place("moved", [P, P, PACK], F32, None)
+                    nc.scalar.copy(moved[e, c][:], turned[e, c][:].rearrange("p j s -> p s j"))
 
         def products(e):
             da[e] = place("da%d" % e, [P, 2, C, PACK], BF16, turn(e))
@@ -197,6 +200,11 @@ def tile_moe_bdx_mlp_relu2_kernel(
                 if c >= FUSED[e]:
                     slope = place("slope%d%d" % (e, c), [P, PACK, P], F32, slopes_at(e) + c * QUARTER)
                     nc.gpsimd.tensor_scalar(slope[:], a_sb[e][:, :, cols], FLOAT_MAX, 0.0, ALU.min, ALU.max)
+                if (e, c) in moved:
+                    nc.gpsimd.tensor_tensor(
+                        da[e][:, 0, cols, :], slope[:].rearrange("p j s -> p s j"), moved[e, c][:], ALU.mult
+                    )
+                elif c >= FUSED[e]:
                     nc.vector.tensor_tensor(
                         da[e][:, 0, cols, :].rearrange("p (c i) j -> p c j i", i=2),
                         slope[:].rearrange("p j (c i) -> p c j i", i=2),
@@ -246,8 +254,8 @@ def tile_moe_bdx_mlp_relu2_kernel(
             nc.sync.dma_start(out[kb * P : (kb + 1) * P, lo:hi], total[:])
 
         def combine(kb, width, firsts_at, totals_at):
-            cuts = range(0, T, width)
-            firsts = [gather_first(kb, lo, lo + width, firsts_at + lo * 4) for lo in cuts]
+            cuts = list(range(0, T, width)) + ([T - P] if width < HALF else [])
+            firsts = [gather_first(kb, lo, hi, firsts_at + lo * 4) for lo, hi in zip(cuts, cuts[1:] + [T])]
             for lo, first in zip(cuts, firsts):
                 gather_second(kb, lo, first, totals_at + lo * 4)
 
@@ -264,6 +272,7 @@ def tile_moe_bdx_mlp_relu2_kernel(
         gather_scales(4, W2_AT + MATRIX)
         gather_words(3, W2_AT + MATRIX + QUARTER)
         products(0)
+        gather_words(E - 1, FIRST_AT + QUARTER)
         for e in range(1, E):
             if e + 1 < E:
                 quantize_w2(e + 1, round_w2(e + 1))
@@ -271,8 +280,6 @@ def tile_moe_bdx_mlp_relu2_kernel(
                 quantize_w1([0, 1], 0, round_w1([0, 1], 0, nc.scalar.copy, turn(e)), slopes_at(e - 1) + 2 * QUARTER)
             first_layer(e)
             quantize_da(e - 1)
-            if e == 1:
-                gather_words(E - 1, FIRST_AT + 3 * QUARTER)
             products(e)
 
         dx = [place("dx%d" % kb, [P, S], F32, W2_AT + kb * S * 4) for kb in range(BLOCKS)]
@@ -289,14 +296,23 @@ def tile_moe_bdx_mlp_relu2_kernel(
         quantize_w1([4], 1, single)
         combine(0, HALF, spare[0], SUMS_AT)
         second_layer(1, usual)
-        far = [round_w1(pair, 2, nc.vector.tensor_copy, turn(2) + n * 2 * QUARTER) for n, pair in enumerate(([0, 1], [2, 3]))]
+        groups = [[0, 1], [2, 3], [4]]
+        far_at = [turn(2), turn(2) + 2 * QUARTER, turn(3)]
+        far = [place("far%d" % n, [P, len(groups[n]) * 2 * P, PACK], BF16, far_at[n]) for n in range(3)]
+
+        def round_far(e):
+            interleave(nc.vector.tensor_copy, far[e // 2][:, e % 2 * 2 * P : (e % 2 + 1) * 2 * P, :], w1_raw[e, 2][:])
+
         last_far = W1_AT + 4 * MATRIX + 2 * QUARTER
-        far.append(round_w1([4], 2, nc.vector.tensor_copy, turn(3)))
-        quantize_w1([0, 1], 2, far[0], W1_AT + 2 * MATRIX + 2 * QUARTER)
-        quantize_w1([2, 3], 2, far[1], last_far + 2624)
-        quantize_w1([4], 2, far[2])
+        for e in range(3):
+            round_far(e)
+        quantize_w1(groups[0], 2, far[0], W1_AT + 2 * MATRIX + 2 * QUARTER)
+        for e in range(3, E):
+            round_far(e)
+        quantize_w1(groups[1], 2, far[1], last_far + 2624)
+        quantize_w1(groups[2], 2, far[2])
         combine(1, HALF, spare[4], last_far - 2496)
         second_layer(2, usual)
         combine(2, HALF, spare[6], spare[8])
-        second_layer(3, ["turned"] * 3 + ["sums"] * 2, on_vector=2)
+        second_layer(3, ["turned"] * 3 + ["sums"] * 2, on_vector=3)
         combine(3, PIECE, spare[0], spare[4])

@@ -296,21 +296,15 @@ def tile_moe_bdx_mlp_relu2_kernel(
         quantize_w1([4], 1, single)
         combine(0, HALF, spare[0], SUMS_AT)
         second_layer(1, usual)
-        groups = [[0, 1], [2, 3], [4]]
-        far_at = [turn(2), turn(2) + 2 * QUARTER, turn(3)]
-        far = [place("far%d" % n, [P, len(groups[n]) * 2 * P, PACK], BF16, far_at[n]) for n in range(3)]
-
-        def round_far(e):
-            interleave(nc.vector.tensor_copy, far[e // 2][:, e % 2 * 2 * P : (e % 2 + 1) * 2 * P, :], w1_raw[e, 2][:])
-
         last_far = W1_AT + 4 * MATRIX + 2 * QUARTER
-        for e in range(3):
-            round_far(e)
-        quantize_w1(groups[0], 2, far[0], W1_AT + 2 * MATRIX + 2 * QUARTER)
-        for e in range(3, E):
-            round_far(e)
-        quantize_w1(groups[1], 2, far[1], last_far + 2624)
-        quantize_w1(groups[2], 2, far[2])
+        for experts, far_at in ((range(E - 1), turn(2)), ([E - 1], turn(3))):
+            width = len(experts) * P
+            far = [place("far%d%d" % (width, h), [P, width, PACK], BF16, far_at + h * width * 8) for h in range(2)]
+            for n, e in enumerate(experts):
+                for h in range(2):
+                    interleave(nc.vector.tensor_copy, far[h][:, n * P : (n + 1) * P, :], w1_raw[e, 2][:, :, h * P : (h + 1) * P])
+            for h in range(2):
+                quantize_w1(list(experts), 2 + h, far[h])
         combine(1, HALF, spare[4], last_far - 2496)
         second_layer(2, usual)
         combine(2, HALF, spare[6], spare[8])

@@ -221,7 +221,7 @@ def tile_moe_bdx_mlp_relu2_kernel(
                         op1=ALU.mult,
                     )
 
-        def second_layer(kb, rings, on_vector=0):
+        def second_layer(kb, rings, on_vector=()):
             accs = []
             for e in range(E):
                 acc = psum.tile([P, C], F32, name=rings[e], tag=rings[e], bufs=4)
@@ -237,7 +237,7 @@ def tile_moe_bdx_mlp_relu2_kernel(
                 )
                 accs.append(acc)
             for e in range(E):
-                copy = nc.vector.tensor_copy if e < on_vector else nc.scalar.copy
+                copy = nc.vector.tensor_copy if e in on_vector else nc.scalar.copy
                 copy(dx[kb][:, e * C : (e + 1) * C], accs[e][:])
 
         spare = [A_AT + e * MATRIX + (1 + h) * 2560 for e in range(E) for h in range(2)]
@@ -289,7 +289,7 @@ def tile_moe_bdx_mlp_relu2_kernel(
         quantize_da(E - 1)
         quantize_w1([4], 0, rounded, last + QUARTER // 2)
         usual = ["sums"] * (E - 1) + ["turned"]
-        second_layer(0, usual)
+        second_layer(0, usual, on_vector=(3,))
         four = round_w1([0, 1, 2, 3], 1, nc.vector.tensor_copy, turn(E - 1) + 2 * QUARTER)
         single = round_w1([4], 1, nc.vector.tensor_copy, turn(E - 1))
         quantize_w1([0, 1, 2, 3], 1, four)
@@ -308,5 +308,5 @@ def tile_moe_bdx_mlp_relu2_kernel(
         combine(1, HALF, spare[4], last_far - 2496)
         second_layer(2, usual)
         combine(2, HALF, spare[6], spare[8])
-        second_layer(3, ["turned"] * 3 + ["sums"] * 2, on_vector=3)
+        second_layer(3, ["turned"] * 3 + ["sums"] * 2, on_vector=(0, 1, 2))
         combine(3, PIECE, spare[0], spare[4])

@@ -50,8 +50,8 @@ def tile_moe_bdx_mlp_relu2_kernel(
 
         def place(name, shape, dtype, offset):
             if offset is None:
-                return keep.tile(shape, dtype, name=name, align_bytes=64)
-            return laid.tile(shape, dtype, name=name, offset=offset, align_bytes=64)
+                return keep.tile(shape, dtype, name=name, align_bytes=256)
+            return laid.tile(shape, dtype, name=name, offset=offset, align_bytes=256)
 
         def turn(e):
             return TURN_AT + e % 3 * MATRIX
@@ -181,7 +181,7 @@ def tile_moe_bdx_mlp_relu2_kernel(
                     stop=True,
                 )
             for c in range(CHUNKS):
-                dh = keep.tile([P, PACK, P], F32, name="dh", bufs=6, align_bytes=64)
+                dh = keep.tile([P, PACK, P], F32, name="dh", bufs=6, align_bytes=256)
                 col = e * CHUNKS + c
                 nc.scalar.activation(
                     dh[:], sums[c][:].rearrange("s (p j) -> s j p", j=PACK), COPY, scale=gate2[:, col : col + 1]
@@ -305,7 +305,7 @@ def tile_moe_bdx_mlp_relu2_kernel(
                     interleave(nc.vector.tensor_copy, far[h][:, n * P : (n + 1) * P, :], w1_raw[e, 2][:, :, h * P : (h + 1) * P])
             for h in range(2):
                 quantize_w1(list(experts), 2 + h, far[h])
-        combine(1, HALF, spare[4], last_far - 2496)
+        combine(1, HALF, spare[4], last_far - 2304)
         second_layer(2, usual)
         combine(2, HALF, spare[6], spare[8])
         second_layer(3, ["turned"] * 3 + ["sums"] * 2, on_vector=(0, 1, 2))

@@ -51,7 +51,7 @@ def tile_moe_bdx_mlp_relu2_kernel(
         def place(name, shape, dtype, offset):
             if offset is None:
                 return keep.tile(shape, dtype, name=name, align_bytes=256)
-            return laid.tile(shape, dtype, name=name, offset=offset, align_bytes=256)
+            return laid.tile(shape, dtype, name=name, offset=offset, align_bytes=256 if offset else QUARTER)
 
         def turn(e):
             return TURN_AT + e % 3 * MATRIX

from contextlib import ExitStack

import concourse.mybir as mybir
from concourse.masks import make_identity

K, T, E, C, H, N = 512, 1280, 5, 512, 512, 512
S = E * C
FLOPS = 2 * S * (N * H + H * K)
BYTES = 128 * T * 4 + 16 * T + 4 * (H * S + E * N * H + E * H * K + S + K * T) + 2 * 128 * (S + 2 * T) // 16

F32 = mybir.dt.float32
BF16 = mybir.dt.bfloat16
I32 = mybir.dt.int32
U32 = mybir.dt.uint32
U16 = mybir.dt.uint16
U8 = mybir.dt.uint8
E4M3 = mybir.dt.float8_e4m3fn_x4
E5M2 = mybir.dt.float8_e5m2_x4
ALU = mybir.AluOpType
COPY = mybir.ActivationFunctionType.Copy

P = 128
PACK = 4
CHUNKS = C // P
BLOCKS = K // P
HALF = T // 2
FLOAT_MAX = 3.4028234663852886e38
FUSED = (0, 2, 2, 2, 2)

MATRIX = 8192
QUARTER = MATRIX // 4
W2_AT = 0
A_AT = W2_AT + E * MATRIX
W1_AT = A_AT + E * MATRIX
FIRST_AT = W1_AT + E * MATRIX
TURN_AT = FIRST_AT + MATRIX
SUMS_AT = TURN_AT + 3 * MATRIX
PIECE = 256


def tile_moe_bdx_mlp_relu2_kernel(
    tc, dy_words, dy_scales, a, w2, w1, gate, offs, pos1, pos2, out
):
    nc = tc.nc
    with ExitStack() as ctx:
        lists = ctx.enter_context(tc.tile_pool(name="lists", bufs=1))
        keep = ctx.enter_context(tc.tile_pool(name="keep", bufs=1))
        laid = ctx.enter_context(tc.tile_pool(name="laid", bufs=1))
        psum = ctx.enter_context(tc.psum_pool(name="psum", bufs=1))

        def place(name, shape, dtype, offset):
            if offset is None:
                return keep.tile(shape, dtype, name=name, align_bytes=256)
            return laid.tile(shape, dtype, name=name, offset=offset, align_bytes=256 if offset else QUARTER)

        def turn(e):
            return TURN_AT + e % 3 * MATRIX

        def slopes_at(e):
            return turn(e - 1) if e else FIRST_AT

        offs_sb = lists.tile([P, S // 16], U16, name="offs_sb")
        pos1_sb = lists.tile([P, T // 16], U16, name="pos1_sb")
        pos2_sb = lists.tile([P, T // 16], U16, name="pos2_sb")
        dy_w = place("dy_w", [P, T], I32, None)
        dy_s = place("dy_s", [P, T], U8, None)
        gate_rows = place("gate_rows", [P, P], F32, None)
        gate2 = place("gate2", [P, S // P], F32, None)
        ident = place("ident", [P, P], F32, None)

        w2_raw, a_sb, w1_raw, moved = {}, {}, {}, {}
        turned, w2_mx, g_words, g_scales, da, da_mx, w1_mx = {}, {}, {}, {}, {}, {}, {}

        def load_w2(e):
            w2_raw[e] = place("w2_raw%d" % e, [P, PACK, H], F32, W2_AT + e * MATRIX)
            nc.sync.dma_start(w2_raw[e][:], w2[e].rearrange("(p j) i -> p j i", j=PACK))

        def load_a(e):
            a_sb[e] = place("a%d" % e, [P, PACK, C], F32, A_AT + e * MATRIX)
            nc.sync.dma_start(a_sb[e][:], a[:, e * C : (e + 1) * C].rearrange("(p j) s -> p j s", j=PACK))

        def load_w1(e, first, last, offset=None):
            offset = W1_AT + e * MATRIX + first * QUARTER if offset is None else offset
            raw = place("w1_raw%d%d" % (e, first), [P, PACK, (last - first) * P], F32, offset)
            nc.sync.dma_start(raw[:], w1[e][:, first * P : last * P].rearrange("(p j) k -> p j k", j=PACK))
            w1_raw[e, first] = raw

        nc.gpsimd.memset(gate_rows[:], 0.0)
        make_identity(nc, ident[:])
        nc.sync.dma_start(offs_sb[:], offs)
        for q in range(4):
            rows = dy_scales[0, 4 * q : 4 * q + 4, :].bitcast(I32)
            nc.sync.dma_start(dy_s[32 * q : 32 * (q + 1), :].bitcast(I32), rows.unsqueeze(0).broadcast_to([8, 4, T // 4]))
        load_w2(0)
        nc.sync.dma_start(dy_w[:], dy_words[0].rearrange("p t d -> p (t d)").bitcast(I32))
        nc.sync.dma_start(gate_rows[0 : S // P, :], gate[0].rearrange("(c s) -> c s", s=P))
        load_w2(1)
        load_w2(2)
        load_a(0)
        load_w2(3)
        load_a(1)
        load_w2(4)
        load_a(2)
        load_a(3)
        load_w1(0, 0, 1)
        load_w1(1, 0, 1)
        load_a(4)
        for e in range(2, E):
            load_w1(e, 0, 1)
        nc.sync.dma_start(pos1_sb[:], pos1)
        nc.sync.dma_start(pos2_sb[:], pos2)
        for e in range(E):
            load_w1(e, 1, 2, SUMS_AT + 1536 if e + 1 == E else None)
        for e in range(E):
            load_w1(e, 2, 4)

        gate_t = psum.tile([P, PACK, P], F32, name="turned", tag="turned", bufs=4)
        nc.tensor.transpose(gate_t[:, 0, :], gate_rows[:], ident[:])

        def interleave(copy, dst, src):
            copy(dst.rearrange("p (c i) j -> p c j i", i=2), src.rearrange("p j (c i) -> p c j i", i=2))

        def quantize(name, rounded, fmt, codes_at, scales_at=None):
            width = rounded.shape[1]
            codes = place(name + "_codes", [P, width], U32, codes_at)
            scales = place(name + "_scales", [P, width], U8, scales_at)
            nc.vector.quantize_mx(out=codes[:].bitcast(fmt), scales=scales[:], in_=rounded.rearrange("p c j -> p (c j)"))
            return codes, scales

        def gather_words(e, offset):
            g_words[e] = place("g_words%d" % e, [P, C], U32, offset)
            nc.vector.tensor_copy(g_words[e][:], dy_w[:].bitcast(U32).indirect(offs_sb[:, e * C // 16 : (e + 1) * C // 16]))

        def gather_scales(e, offset):
            g_scales[e] = place("g_scales%d" % e, [P, C], U8, offset)
            nc.vector.tensor_copy(g_scales[e][:], dy_s[:].indirect(offs_sb[:, e * C // 16 : (e + 1) * C // 16]))

        def round_w2(e, on_gpsimd=False):
            rounded = place("w2_bf%d" % e, [P, H, PACK], BF16, turn(max(e - 1, 0)))
            for h in range(2):
                cols = slice(h * H // 2, (h + 1) * H // 2)
                if on_gpsimd:
                    nc.gpsimd.tensor_scalar(
                        rounded[:, cols, :], w2_raw[e][:, :, cols].rearrange("p j c -> p c j"), 1.0, 0.0, ALU.mult, ALU.add
                    )
                else:
                    interleave(nc.scalar.copy, rounded[:, cols, :], w2_raw[e][:, :, cols])
            return rounded

        def quantize_w2(e, rounded):
            w2_mx[e] = quantize("w2_%d" % e, rounded[:], E4M3, slopes_at(e - 2) + 2 * QUARTER if e >= 2 else None)

        def round_w1(experts, kb, copy, rounded_at):
            width = w1_raw[experts[0], kb].shape[2]
            rounded = place("w1_bf%d%d" % (kb, experts[0]), [P, len(experts) * width, PACK], BF16, rounded_at)
            for n, e in enumerate(experts):
                interleave(copy, rounded[:, n * width : (n + 1) * width, :], w1_raw[e, kb][:])
            return rounded

        def quantize_w1(experts, kb, rounded, codes_at=None):
            codes, scales = quantize("w1_%d%d" % (kb, experts[0]), rounded[:], E4M3, codes_at)
            blocks = rounded.shape[1] // P // len(experts)
            for n in range(rounded.shape[1] // P):
                cols = slice(n * P, (n + 1) * P)
                w1_mx[experts[n // blocks], kb + n % blocks] = codes[:, cols], scales[:, cols]

        def quantize_da(e):
            da_mx[e] = quantize("da%d" % e, da[e][:, 0], E5M2, A_AT + e * MATRIX, A_AT + e * MATRIX + QUARTER)

        def first_layer(e):
            sums = [psum.tile([P, H], F32, name="sums", tag="sums", bufs=4) for c in range(CHUNKS)]
            for c in range(CHUNKS):
                cols = slice(c * P, (c + 1) * P)
                nc.tensor.matmul_mx(
                    out=sums[c][:],
                    lhsT=g_words[e][:, cols].bitcast(E5M2),
                    lhsT_scale=g_scales[e][:, cols],
                    rhs=w2_mx[e][0][:].bitcast(E4M3),
                    rhs_scale=w2_mx[e][1][:],
                    start=True,
                    stop=True,
                )
            for c in range(CHUNKS):
                dh = keep.tile([P, PACK, P], F32, name="dh", bufs=6, align_bytes=256)
                col = e * CHUNKS + c
                nc.scalar.activation(
                    dh[:], sums[c][:].rearrange("s (p j) -> s j p", j=PACK), COPY, scale=gate2[:, col : col + 1]
                )
                turned[e, c] = psum.tile([P, PACK, P], F32, name="turned", tag="turned", bufs=4)
                for j in range(PACK):
                    nc.tensor.transpose(turned[e, c][:, j, :], dh[:, j, :], ident[:])
                if (e, c) == (0, CHUNKS - 1):
                    moved[e, c] = place("moved", [P, P, PACK], F32, None)
                    nc.scalar.copy(moved[e, c][:], turned[e, c][:].rearrange("p j s -> p s j"))

        def products(e):
            da[e] = place("da%d" % e, [P, 2, C, PACK], BF16, turn(e))
            for c in range(CHUNKS):
                cols = slice(c * P, (c + 1) * P)
                if c >= FUSED[e]:
                    slope = place("slope%d%d" % (e, c), [P, PACK, P], F32, slopes_at(e) + c * QUARTER)
                    nc.gpsimd.tensor_scalar(slope[:], a_sb[e][:, :, cols], FLOAT_MAX, 0.0, ALU.min, ALU.max)
                if (e, c) in moved:
                    nc.gpsimd.tensor_tensor(
                        da[e][:, 0, cols, :], slope[:].rearrange("p j s -> p s j"), moved[e, c][:], ALU.mult
                    )
                elif c >= FUSED[e]:
                    nc.vector.tensor_tensor(
                        da[e][:, 0, cols, :].rearrange("p (c i) j -> p c j i", i=2),
                        slope[:].rearrange("p j (c i) -> p c j i", i=2),
                        turned[e, c][:].rearrange("p j (c i) -> p c j i", i=2),
                        ALU.mult,
                    )
                else:
                    nc.vector.scalar_tensor_tensor(
                        out=da[e][:, 0, cols, :],
                        in0=a_sb[e][:, :, cols].rearrange("p j s -> p s j"),
                        scalar=0.0,
                        in1=turned[e, c][:].rearrange("p j s -> p s j"),
                        op0=ALU.max,
                        op1=ALU.mult,
                    )

        def second_layer(kb, rings, on_vector=()):
            accs = []
            for e in range(E):
                acc = psum.tile([P, C], F32, name=rings[e], tag=rings[e], bufs=4)
                codes, scales = w1_mx[e, kb]
                nc.tensor.matmul_mx(
                    out=acc[:],
                    lhsT=codes.bitcast(E4M3),
                    lhsT_scale=scales,
                    rhs=da_mx[e][0][:].bitcast(E5M2),
                    rhs_scale=da_mx[e][1][:],
                    start=True,
                    stop=True,
                )
                accs.append(acc)
            for e in range(E):
                copy = nc.vector.tensor_copy if e in on_vector else nc.scalar.copy
                copy(dx[kb][:, e * C : (e + 1) * C], accs[e][:])

        spare = [A_AT + e * MATRIX + (1 + h) * 2560 for e in range(E) for h in range(2)]

        def gather_first(kb, lo, hi, offset):
            first = place("first%d_%d" % (kb, lo), [P, hi - lo], F32, offset)
            nc.scalar.activation(first[:], dx[kb][:].indirect(pos1_sb[:, lo // 16 : hi // 16]), COPY)
            return first

        def gather_second(kb, lo, first, offset):
            hi = lo + first.shape[1]
            total = place("total%d_%d" % (kb, lo), [P, hi - lo], F32, offset)
            nc.vector.tensor_tensor(total[:], dx[kb][:].indirect(pos2_sb[:, lo // 16 : hi // 16]), first[:], ALU.add)
            nc.sync.dma_start(out[kb * P : (kb + 1) * P, lo:hi], total[:])

        def combine(kb, width, firsts_at, totals_at):
            cuts = list(range(0, T, width)) + ([T - P] if width < HALF else [])
            firsts = [gather_first(kb, lo, hi, firsts_at + lo * 4) for lo, hi in zip(cuts, cuts[1:] + [T])]
            for lo, first in zip(cuts, firsts):
                gather_second(kb, lo, first, totals_at + lo * 4)

        for e in range(3):
            gather_scales(e, None)
        gather_words(0, None)
        quantize_w2(0, round_w2(0))
        nc.scalar.activation(gate2[:], gate_t[:, 0, 0 : S // P], COPY, scale=2.0)
        gather_words(1, W2_AT)
        gather_scales(3, W2_AT + QUARTER)
        gather_words(2, W2_AT + 2 * QUARTER)
        first_layer(0)
        quantize_w2(1, round_w2(1, on_gpsimd=True))
        gather_scales(4, W2_AT + MATRIX)
        gather_words(3, W2_AT + MATRIX + QUARTER)
        products(0)
        gather_words(E - 1, FIRST_AT + QUARTER)
        for e in range(1, E):
            if e + 1 < E:
                quantize_w2(e + 1, round_w2(e + 1))
            else:
                quantize_w1([0, 1], 0, round_w1([0, 1], 0, nc.scalar.copy, turn(e)), slopes_at(e - 1) + 2 * QUARTER)
            first_layer(e)
            quantize_da(e - 1)
            products(e)

        dx = [place("dx%d" % kb, [P, S], F32, W2_AT + kb * S * 4) for kb in range(BLOCKS)]
        last = slopes_at(E - 1) + 2 * QUARTER
        quantize_w1([2, 3], 0, round_w1([2, 3], 0, nc.scalar.copy, FIRST_AT), last)
        rounded = round_w1([4], 0, nc.scalar.copy, FIRST_AT + QUARTER)
        quantize_da(E - 1)
        quantize_w1([4], 0, rounded, last + QUARTER // 2)
        usual = ["sums"] * (E - 1) + ["turned"]
        second_layer(0, usual, on_vector=(3,))
        four = round_w1([0, 1, 2, 3], 1, nc.vector.tensor_copy, turn(E - 1) + 2 * QUARTER)
        single = round_w1([4], 1, nc.vector.tensor_copy, turn(E - 1))
        quantize_w1([0, 1, 2, 3], 1, four)
        quantize_w1([4], 1, single)
        combine(0, HALF, spare[0], SUMS_AT)
        second_layer(1, usual)
        last_far = W1_AT + 4 * MATRIX + 2 * QUARTER
        for experts, far_at in ((range(E - 1), turn(2)), ([E - 1], turn(3))):
            width = len(experts) * P
            far = [place("far%d%d" % (width, h), [P, width, PACK], BF16, far_at + h * width * 8) for h in range(2)]
            for n, e in enumerate(experts):
                for h in range(2):
                    interleave(nc.vector.tensor_copy, far[h][:, n * P : (n + 1) * P, :], w1_raw[e, 2][:, :, h * P : (h + 1) * P])
            for h in range(2):
                quantize_w1(list(experts), 2 + h, far[h])
        combine(1, HALF, spare[4], last_far - 2304)
        second_layer(2, usual)
        combine(2, HALF, spare[6], spare[8])
        second_layer(3, ["turned"] * 3 + ["sums"] * 2, on_vector=(0, 1, 2))
        combine(3, PIECE, spare[0], spare[4])
